import numpy as np, ml_dtypes
CORES = [5,29,101,125,133,157,229,253]
N = 8
import mx_ref
BF = ml_dtypes.bfloat16
def gentries(a):
    return np.ascontiguousarray(a.reshape(8, 16, -1).transpose(0, 2, 1)).reshape(8, -1)
def gtable(e):
    e = np.asarray(e); return np.ascontiguousarray(e.reshape(8, -1, 16).transpose(0, 2, 1)).reshape(128, -1).astype(np.int32)
def gcols(t, e):
    v = np.concatenate([t.reshape(8, 16, -1, 4), np.zeros((8, 16, 1, 4), BF)], axis=2)
    return np.ascontiguousarray(np.stack([v[g][:, e[g]] for g in range(8)])).reshape(128, -1)
def tile(rs):
    return np.stack(rs, axis=2).reshape(128, -1).astype(BF)
def pick(q, e):
    c = np.concatenate([q[0].reshape(128, -1, 4), np.zeros((128, 1, 4), np.uint8)], axis=1); s = np.concatenate([q[1], np.ones((16, 1), np.uint8)], axis=1)
    return (np.ascontiguousarray(c[:, e].reshape(128, -1)), np.ascontiguousarray(s[:, e]))
def join(*qs):
    return (np.concatenate([q[0] for q in qs], axis=1), np.concatenate([q[1] for q in qs], axis=1))
def put(q, e, v):
    c, s = q[0].reshape(128, -1, 4).copy(), q[1].copy(); c[:, e] = v[0].reshape(128, -1, 4); s[:, e] = v[1]
    return (c.reshape(128, -1), s)
def pk(c, s):
    return (np.ascontiguousarray(c), mx_ref.live(s))
def emit(q):
    return q[0], q[1]
def packed(v, rng):
    q = [mx_ref.quantize(np.ascontiguousarray(v[r])) for r in range(N)]
    return np.stack([a for a, b in q]), np.stack([mx_ref.plane(b, rng) for a, b in q])
def values_of_codes():
    e, c = np.zeros((128, 128, 4), np.float32), np.zeros((128, 2, 4), np.uint8)
    e[np.arange(128), np.arange(128), 0] = 1
    c[:127, :, 0] = np.arange(256).reshape(2, 128).T[:127]
    return mx_ref.matmul(mx_ref.quantize(e.reshape(128, 512).astype(BF)), (c.reshape(128, 8), np.full((16, 2), 127, np.uint8))).T.reshape(-1).astype(np.float64)
CODE_VALUE, SCALE_VALUE = values_of_codes(), 2.0 ** (np.arange(256) - 127.0)
def decode(q):
    return (CODE_VALUE[q[0]].reshape(16, 8, -1, 4) * SCALE_VALUE[q[1]][:, None, :, None] + 0.0).reshape(128, -1).astype(np.float32)
def f(rng, *shape):
    return mx_ref.flush((rng.standard_normal(shape, dtype=np.float32) * np.exp2(rng.integers(-2, 3, shape[:-1] + (1,)))).astype(BF))
def wide(rng, *shape, cols=0):
    v = rng.standard_normal(shape, dtype=np.float32) * np.exp2(rng.integers(-12, 13, shape)).astype(np.float32)
    if cols: v *= np.repeat(np.exp2(rng.integers(-cols, cols + 1, shape[:-2] + (1, shape[-1] // 4))) * (rng.random(shape[:-2] + (1, shape[-1] // 4)) > 0.0625), 4, axis=-1).astype(np.float32)
    return mx_ref.flush(v.astype(BF))
C = 320
STEP = [4, 1, 2]
def numbers_of(rng):
    return {"x": np.array(f(rng, N, 128, 4 * C)), "u": np.array(f(rng, N, 128, 512)), "v": np.array(f(rng, N, 128, 512))}
def stored(a, b):
    return {"lam": np.stack([gtable(a[r]) for r in range(N)]), "rho": np.stack([gtable(b[r]) for r in range(N)])}
def dealt(rng):
    e = np.tile(np.arange(C), (N, 8, 1))
    return np.stack([rng.permuted(e, axis=2), rng.permuted(e, axis=2)], axis=3).reshape(N, 8, 2 * C)
def lists(rng):
    a = dealt(rng)
    return stored(a, dealt(rng))
def layers(rng):
    return np.array(f(rng, N, 128, 2048)).reshape(N, 8, 16, 4, 8, 16, 4)
def weights(rng, w):
    c, p = packed(np.ascontiguousarray(w).reshape(N, 128, 2048), rng)
    return {"wc": c, "ws": p}
def unread(u):
    u = u.reshape(N, 128, 128, 4)
    u[:, :, ::16] = 0
    u[:, :, 1::16] = 0
    return u
def setup_inputs(rng):
    return {**numbers_of(rng), **lists(rng), **weights(rng, layers(rng))}
def setup_inputs_ties(rng):
    d = numbers_of(rng)
    o = rng.permutation(N)
    s = rng.integers(-1, 2, (N, 8, 2, C)).astype(np.float32)
    s[o[1]] = 1
    s[o[2]] = -1
    x = d["x"].reshape(N, 8, 16, C, 4)
    x[:, :, :2] = 0
    x[:, :, :2, :, 0] = s.astype(BF)
    c = np.ones(N, np.float32)
    c[o[0]] = 0
    u = unread(d["u"])
    for h in range(0, 128, 16):
        for i in range(2): u[:, h + i, h + i, 0] = c.astype(BF)
    w = layers(rng)
    w[:, :, :, :, :, :8] = 0
    for g in range(8): w[:, g, 15, 0, g, 15, 0] = 2.0 ** 8
    return {"x": x.reshape(N, 128, 4 * C), "u": u.reshape(N, 128, 512), "v": d["v"], **lists(rng), **weights(rng, w)}
def setup_inputs_near(rng):
    d = numbers_of(rng)
    lo = np.unique(np.minimum(np.arange(N), np.arange(N) ^ STEP[0]))
    o = np.zeros(N, np.int64)
    o[lo] = rng.permutation(N // 2) % 2
    o[lo ^ STEP[0]] = o[lo]
    k = np.where(o == 0, 2.0 ** -30, 1.0).astype(np.float32)
    some = rng.permutation(8)[:4]
    x = d["x"].astype(np.float32).reshape(N, 8, 16, C, 4)
    x[:, :, :8] = 0
    x[:, some, 8:] = 0
    for g in some: x[:, g, 15, :, 0] = k[:, None]
    for i in range(2):
        s = rng.integers(-1, 2, (N, 8, C)) * k[:, None, None]
        x[:, :, 2 * i, :, 0] = 1.125 * s
        x[:, :, 2 * i + 1, :, 0] = -1.25 * s
        x[:, :, 6, :, i] = rng.choice([-1.0, 1.0], (N, 8, C)) * k[:, None, None]
        x[:, :, 6, :, 2 + i] = rng.choice([-1.0, 1.0], (N, 8, C)) * k[:, None, None]
    x[:, :, 7, :, 0] = k[:, None, None]
    for r in range(N):
        for g in rng.permutation(8)[:4]: x[r, g, 2 * rng.integers(2), rng.integers(C), 0] = 2.0 ** 30 * rng.choice([-1.0, 1.0])
    u = unread(d["u"])
    for h in range(0, 128, 16):
        for i in range(2):
            u[:, h + 2 * i, h + i, 0] = (1.125 * k).astype(BF)
            u[:, h + 2 * i + 1, h + i, 0] = k.astype(BF)
            u[:, h + 4 + i, h + i, 0] = k.astype(BF)
    w = layers(rng)
    w[:, :, :8] = 0
    w[:, :, :, :, :, :8] = 0
    w[:, :8] = 0
    for g in range(8):
        for i in range(2): w[:, g, 6, 0, g, 4 + i, i] = 2.0 ** -8
        w[:, g, 7, 0, g, 7, 0] = 32.0
    for g in some:
        for i in range(2):
            u[:, 16 * g + 8 + 2 * i, 16 * g + i, 0] = (1.125 * k).astype(BF)
            u[:, 16 * g + 9 + 2 * i, 16 * g + i, 0] = k.astype(BF)
            w[:, g, 6, 0, g, 8 + 2 * i, 2 + i] = 1.125 * 2.0 ** -8
            w[:, g, 6, 0, g, 9 + 2 * i, 2 + i] = -1.25 * 2.0 ** -8
        w[:, g, 7, 0, g, 14, 0] = 32.0
    return {"x": x.reshape(N, 128, 4 * C).astype(BF), "u": u.reshape(N, 128, 512), "v": d["v"], **lists(rng), **weights(rng, w)}
def setup_inputs_odd(rng):
    d = numbers_of(rng)
    x = d["x"].astype(np.float32).reshape(N, 8, 16, C, 4)
    x[:, :, 8:] = 0
    x[:, :, 0, :, 0] = 1.96875 * 2.0 ** 8
    for i in range(2):
        x[:, :, 1 + 2 * i, :, 0] = 2.0 ** -5
        x[:, :, 2 + 2 * i, :, 0] = (7 + 2 * rng.integers(0, 2, (N, 8, C))) * 2.0 ** -8
    x[:, :, 8, :, 0] = -1.125
    x[:, :, 10, :, 0] = 0.0703125 * rng.choice([-1.0, 1.0], (N, 8, C))
    u = unread(d["u"])
    for h in range(0, 128, 16):
        for i in range(2):
            c = rng.choice([-1.0, 1.0], N).astype(np.float32)
            u[:, h + 1 + 2 * i, h + i, 0] = c.astype(BF)
            u[:, h + 2 + 2 * i, h + i, 0] = (-1.125 * c).astype(BF)
    w = np.zeros((N, 8, 16, 4, 8, 16, 4), np.float32)
    for g in range(8):
        w[:, g, 8, 0, g, 8, 0] = -28.0
        w[:, g, 2, 0, g, 12, 0] = 32.0
        for b in range(4): w[:, g, 10, b, g, 9, 0] = -2.0 ** (b - 5)
    return {"x": x.reshape(N, 128, 4 * C).astype(BF), "u": u.reshape(N, 128, 512), "v": d["v"], **lists(rng), **weights(rng, w.astype(BF))}
def setup_inputs_ends(rng):
    d = numbers_of(rng)
    o, e = rng.permutation(N) % 4, rng.permutation(N) % 4
    s = rng.choice([-1.0, 1.0], (N, 128, C, 4))
    s[o == 0] = -1
    s[o == 1] = rng.choice([-1.0, 1.0], (N, 1, C, 1))[o == 1]
    x = s * (0.93 + 0.02 * rng.random((N, 128, C, 4))) * 2.0 ** 30
    x[o == 3] = 2.0 ** -30
    size = np.where(o == 3, 2.0 ** -30, 2.0 ** 30)
    u = unread(d["u"])
    for r in range(N):
        h = rng.permutation(8)
        for i in range(2):
            c = np.where(h < 2, 0.0, ((h >> i) % 2) * 2.0 - 1.0) * size[r]
            u[r, :, i::16] = c.astype(np.float32).astype(BF)[None, :, None]
    v = rng.choice([-1.0, 1.0], (N, 128, 512)) * np.where(o < 2, 2.0 ** 30, 2.0 ** -30)[:, None, None]
    t = rng.integers(0, C, (2, N, 8, 2 * C))
    t[:, e == 0] = C - 1
    t[:, e == 1] = 0
    t[:, e == 2] = np.arange(2 * C) % 2 * (C - 1)
    w = np.zeros((N, 128, 4, 128, 4), np.float32)
    j = np.arange(127)
    for b in range(4): w[:, j, b, j, b] = np.array([-0.25, -0.25, -2.0 ** -8, 32.0])[o][:, None]
    return {"x": x.astype(np.float32).reshape(N, 128, 4 * C).astype(BF), "u": u.reshape(N, 128, 512), "v": v.astype(np.float32).astype(BF), **stored(t[0], t[1]), **weights(rng, w.astype(BF))}
def setup_inputs_spread(rng):
    d = setup_inputs(rng)
    d["x"] = wide(rng, N, 128, 4 * C, cols=6)
    return d
def check_inputs(d):
    b = []
    for k in ("x", "u", "v"):
        a = np.abs(d[k].astype(np.float32))
        if not (np.isfinite(a).all() and ((a == 0) | (a >= 2.0 ** -30) & (a <= 2.0 ** 30)).all()): b.append("a value of " + k)
    for k in ("lam", "rho"):
        if not ((d[k] >= 0) & (d[k] < C)).all(): b.append("an entry of " + k)
    none, least, most = [emit(mx_ref.quantize(np.full((128, 16), k, np.float32).astype(BF)))[1][0, 0] for k in (0.0, 2.0 ** -8, 2.0 ** 8)]
    for r in range(N):
        if ((d["wc"][r] == 0x7F) | (d["wc"][r] == 0xFF)).any(): b.append("wc: a code that is no number")
        s = mx_ref.live(d["ws"][r])
        if ((s != none) & ((s < least) | (s > most))).any(): b.append("ws: a scale out of range")
        if (((d["wc"][r].reshape(16, 8, 512, 4) & 0x7F) != 0) & (s == none)[:, None, :, None]).any(): b.append("wc: a code other than zero under the scale of zeros")
    return b
def swapped(t, where):
    a = t.reshape(8, C, 2)
    return np.where(where[:, :, None], a[:, :, ::-1], a).reshape(8, 2 * C)
def reference(x, u, v, lam, rho, wc, ws):
    qu = [mx_ref.quantize(u[r]) for r in range(N)]
    lay = [pk(wc[r], ws[r]) for r in range(N)]
    left, right = [gentries(lam[r]) for r in range(N)], [gentries(rho[r]) for r in range(N)]
    now = [x[r] for r in range(N)]
    q = [mx_ref.quantize(now[r]) for r in range(N)]
    s = [mx_ref.matmul(qu[r], q[r]) for r in range(N)]
    for step in STEP:
        at, mid, sent = [], [], []
        for r in range(N):
            bit = (s[r][::16] > 0).astype(np.int64)
            up, down = np.zeros((8, C), np.int64), np.zeros((8, C), np.int64)
            up[0] = np.arange(C)
            down[7] = np.arange(C)
            for g in range(7):
                up[g + 1] = left[r][g][2 * up[g] + bit[g]]
            for g in range(7, 0, -1):
                down[g - 1] = right[r][g][2 * down[g] + bit[g]]
            at.append(np.take_along_axis(up, down, axis=1))
            mid.append(((now[r].astype(np.float32) + gcols(now[r], at[r]).astype(np.float32)) * np.float32(0.5)).astype(BF))
            z = mx_ref.quantize(mid[r])
            sent.append(mx_ref.quantize(tile([mx_ref.matmul(pick(lay[r], np.arange(128 * b, 128 * b + 128)), z) * np.float32(0.03125) for b in range(4)])))
        for r in range(N):
            p = r ^ step
            far = gcols(decode(sent[p]).astype(BF), np.take_along_axis(at[p], at[r], axis=1))
            now[r] = (mid[r].astype(np.float32) + far.astype(np.float32)).astype(BF)
            q[r] = mx_ref.quantize(now[r])
            s[r] = mx_ref.matmul(qu[r], q[r])
            left[r], right[r] = swapped(left[r], s[r][1::16] < 0), swapped(right[r], s[r][1::16] > 0)
    y, lr = np.zeros((N, 128, C), np.float32), np.zeros((N, 8, 4 * C), np.float32)
    oc, osc = np.zeros((N, 128, 4 * C), np.uint8), np.zeros((N, 16, C), np.uint8)
    for r in range(N):
        y[r] = mx_ref.matmul(mx_ref.quantize(v[r]), q[r])
        lr[r] = np.concatenate([left[r], right[r]], axis=1)
        oc[r], osc[r] = emit(q[r])
    return {"y": y, "lr": lr, "oc": oc, "osc": osc}

@@ -1,0 +1,614 @@
+from concourse.bass import DstId, RemoteDMATransfer
+from concourse.mybir import dt, AluOpType, ActivationFunctionType
+import comms_topo
+
+OP = AluOpType
+AF = ActivationFunctionType
+STEP = [4, 1, 2]
+BIG = 1.0e6
+EPS = 2.0 ** -93
+
+F, B, I, U, C4, S8 = "float32", "bfloat16", "int32", "uint16", "float8_e4m3fn_x4", "uint8"
+SCRATCH = {"ps": ("psum", [128, 4096], F)}
+for _n, _w, _d in [
+    ("x0", 1280, B), ("x1", 1280, B), ("x2", 1280, B), ("x3", 1280, B), ("xh", 1280, B), ("xg", 1280, B), ("vt", 1280, B), ("ht", 1280, B), ("dd", 1280, B),
+    ("ub", 512, B), ("vb", 512, B), ("et", 2048, B), ("ones", 512, B),
+    ("uq", 128, C4), ("us", 128, S8), ("vq", 128, C4), ("vs", 128, S8), ("wq", 512, C4), ("wsp", 512, S8),
+    ("utq", 128, C4), ("uts", 128, S8), ("ufq", 768, C4), ("ufs", 768, S8), ("eq", 512, C4), ("es", 512, S8),
+    ("qx0", 320, C4), ("sx0", 320, S8), ("qx1", 320, C4), ("sx1", 320, S8), ("qx2", 320, C4), ("sx2", 320, S8), ("qx3", 320, C4), ("sx3", 320, S8),
+    ("qv", 320, C4), ("qvs", 320, S8),
+    ("qh1", 320, C4), ("sh1", 320, S8), ("qh2", 320, C4), ("sh2", 320, S8), ("qh3", 320, C4), ("sh3", 320, S8),
+    ("lq1", 320, C4), ("ls1", 320, S8), ("lq2", 320, C4), ("ls2", 320, S8), ("lq3", 320, C4), ("ls3", 320, S8), ("rlq", 320, C4), ("rls", 320, S8),
+    ("nl", 320, I), ("nlu", 320, U), ("tw", 5120, F), ("nw", 3840, B), ("sg2", 1920, B), ("w4", 320, F),
+    ("jj", 320, I), ("jk", 320, I), ("mask", 320, F), ("rs", 320, F), ("rb", 800, F), ("st", 320, F),
+    ("cid", 16, F), ("dva", 16, F), ("dvb", 16, F), ("ea", 16, F), ("da", 16, F), ("eb", 16, F), ("db", 16, F), ("tmp", 256, F),
+    ("y1", 160, F), ("y1s", 160, F), ("y2i", 160, F), ("y2b", 160, F), ("y2", 960, F), ("y2s", 960, F), ("ye", 640, F), ("yes", 640, F),
+    ("lu", 128, U), ("nu", 128, U), ("lt0", 16, F), ("lt1", 16, F), ("bc0", 320, B), ("bc1", 320, B), ("lw", 640, B), ("km", 320, B), ("kt", 320, B),
+    ("mlu", 32, U), ("of", 128, U), ("kl1", 20, U), ("kl2", 20, U), ("kl3", 20, U), ("kr1", 20, U), ("kr2", 20, U), ("kr3", 20, U), ("rlk", 20, U),
+    ("kw", 320, F), ("ky", 320, F), ("kys", 320, F), ("mo", 128, U),
+    ("sn", 320, F), ("fn", 20, F), ("ltb", 40, F), ("rtb", 40, F), ("lrow", 640, F), ("rrow", 640, F), ("lni", 80, I), ("lnu", 80, U), ("lout", 80, F), ("lt2", 64, F),
+    ("yb", 320, F), ("sgc", 8, F), ("sgn", 8, F), ("cli", 64, I), ("clu", 64, U), ("ui", 64, I), ("uf", 64, F), ("uoff", 64, U), ("qi", 16, I), ("qf", 128, F),
+]:
+    SCRATCH[_n] = ("sbuf", [128, _w], _d)
+
+SEMAPHORES = (["sv", "sa", "st", "sg", "dx0", "dx1", "du", "dv", "dw", "dl", "dt0", "dt1", "fn1", "fn2", "fn3", "oy", "ol", "oq0", "oq1", "lsem", "ry0", "ry1", "rk"]
+              + ["dn%d" % s for s in range(8)] + ["ar%d%d" % (r, h) for r in (1, 2, 3) for h in (0, 1)] + ["kr%d" % r for r in (1, 2, 3)])
+
+
+def bits_of(engines):
+    m = 0
+    for e in engines:
+        m |= 1 << e
+    return m
+
+
+def relays_of(core, dst, topo):
+    c = [k for k in topo.cores_of(core) if k != core and topo.may_write(k, dst)]
+    return [[k for k in c if topo.die(k) == topo.die(core)][0], [k for k in c if topo.die(k) != topo.die(core)][0]]
+
+
+def relay_program(g, core, T, topo):
+    for r, src in enumerate(T.cores):
+        dst = T.cores[r ^ STEP[1]]
+        if core not in topo.cores_of(src) or core == src:
+            continue
+        rel = relays_of(src, dst, topo)
+        if core not in rel:
+            continue
+        k = rel.index(core)
+        rid, pid = topo.addr(dst, core)
+        m, n = topo.mask(core, dst), len(topo.engines(core, dst))
+        half = len(topo.engines(src, core)) // 2
+        sent = 0
+        if k == 0:
+            g.wait_ge(T.sem.rk, half)
+            g.remote_dma(T.kr2[:], T.rlk[:], T.sem.kr2, T.sem.lsem, pid, rid, m)
+            sent += n
+        for h in (0, 1):
+            a = 160 * h + 80 * k
+            g.wait_ge(T.sem["ry%d" % h], 2 * half)
+            g.remote_dma(T.lq2[:, a:a + 80].bitcast(dt.uint8), T.rlq[:, a:a + 80].bitcast(dt.uint8), T.sem["ar2%d" % h], T.sem.lsem, pid, rid, m)
+            g.remote_dma(T.ls2[:, a:a + 80], T.rls[:, a:a + 80], T.sem["ar2%d" % h], T.sem.lsem, pid, rid, m)
+            sent += 2 * n
+        g.wait_ge(T.sem.lsem, sent)
+
+
+def table_of(a, s):
+    if s < 6:
+        return ("l", s + 1) if s < 2 * a else ("r", 6 - s + 2 * a)
+    return ("r", 7) if (s == 6) == (a == 0) else ("l", 0)
+
+
+def rank_program(g, core, T, topo):
+    rank = T.rank_of(core)
+    if rank is None:
+        relay_program(g, core, T, topo)
+        return
+    Q = {"g": g, "v": g.vector, "a": g.scalar, "t": g.tensor, "s": g.sync}
+    SEM = {"g": "sg", "v": "sv", "a": "sa", "t": "st"}
+    total, waited, wrote, reads = {}, {}, {}, {}
+
+    def need(q, deps):
+        for sem in sorted(deps):
+            if waited.get((q, sem), 0) < deps[sem]:
+                waited[(q, sem)] = deps[sem]
+                Q[q].wait_ge(T.sem[sem], deps[sem])
+
+    def deps_of(r, w):
+        d = {}
+        for k in list(r) + list(w):
+            if k in wrote:
+                d[wrote[k][0]] = max(d.get(wrote[k][0], 0), wrote[k][1])
+        for k in w:
+            for sem, v in reads.get(k, {}).items():
+                d[sem] = max(d.get(sem, 0), v)
+        return d
+
+    def note(sem, r, w):
+        for k in r:
+            reads.setdefault(k, {})[sem] = total[sem]
+        for k in w:
+            wrote[k] = (sem, total[sem])
+            reads[k] = {}
+
+    def op(q, fn, r, w):
+        need(q, deps_of(r, w))
+        sem = SEM[q]
+        if q == "g" and total.get(sem, 0):
+            need(q, {sem: total[sem]})
+        fn(Q[q]).then_inc(T.sem[sem], 1)
+        total[sem] = total.get(sem, 0) + 1
+        note(sem, r, w)
+
+    def dma(q, pairs, r, w, sem):
+        need(q, deps_of(r, w))
+        for o, i in pairs:
+            Q[q].dma_start(o, i).then_inc(T.sem[sem], 16)
+            total[sem] = total.get(sem, 0) + 16
+        note(sem, r, w)
+
+    def tt(o, a, b, f, r, w):
+        op("v", lambda e: e.tensor_tensor(o, a, b, f), r, w)
+
+    def ts(o, a, s1, s2, f1, f2, r, w):
+        if f2 is None:
+            op("v", lambda e: e.tensor_scalar(o, a, s1, None, f1), r, w)
+        else:
+            op("v", lambda e: e.tensor_scalar(o, a, s1, s2, f1, f2), r, w)
+
+    def lin(o, a, m, b, r, w):
+        ts(o, a, float(m), float(b), OP.mult, OP.add, r, w)
+
+    def cp(o, a, r, w, q="v"):
+        if q == "v":
+            op("v", lambda e: e.tensor_copy(o, a), r, w)
+        else:
+            op("a", lambda e: e.activation(o, a, AF.Copy), r, w)
+
+    def tr(o, a, r, w):
+        op("v", lambda e: e.transpose(o, a), r, w)
+
+    def scan(o, d0, d1, f0, f1, r, w):
+        op("v", lambda e: e.tensor_tensor_scan(o, d0, d1, BIG, f0, f1), r, w)
+
+    def mm(bank, n, lq, lsc, rq, rsc, r):
+        op("t", lambda e: e.matmul_mx(T.ps[:, 512 * bank:512 * bank + n], lq, lsc, rq, rsc, True, True), r, ["b%d" % bank])
+
+    def fill(o, c, w):
+        op("v", lambda e: e.memset(o, c), [], w)
+
+    def quant(q, s, t, r, w):
+        op("v", lambda e: e.quantize_mx(q, s, t), r, w)
+
+    def bank(b, n):
+        return T.ps[:, 512 * b:512 * b + n]
+
+    mask1, rst1 = T.mask[:, 0:160], T.rs[:, 0:160]
+
+    for h in (0, 1):
+        dma("s", [(T.x0[:, 640 * h:640 * h + 640], T.x[:, 640 * h:640 * h + 640])], [], ["x0%d" % h], "dx%d" % h)
+    dma("a", [(T.ub[:], T.u[:])], [], ["ub"], "du")
+    for k, s in enumerate((6, 0, 7, 1, 2, 3, 4, 5)):
+        pairs = []
+        for a in range(4):
+            side, gr = table_of(a, s)
+            src = (T.lam if side == "l" else T.rho)[16 * gr:16 * gr + 16, :]
+            for b in (0, 1):
+                p = 16 * (2 * a + b)
+                pairs.append((T.nl[p:p + 16, 40 * s:40 * s + 40], src))
+        dma("s" if k % 2 == 0 else "a", pairs, [], ["nl%d" % s], "dn%d" % s)
+    dma("s", [(T.wq[:].bitcast(dt.uint8), T.wc[:]), (T.wsp[:], T.ws[:])], [], ["wq"], "dw")
+    dma("s", [(T.lni[:, 0:40], T.lam[:]), (T.lni[:, 40:80], T.rho[:])], [], ["lni"], "dl")
+    dma("s", [(T.vb[:], T.v[:])], [], ["vb"], "dv")
+
+    def iota(o, pattern, base, cm, w, fl=False):
+        if fl:
+            op("g", lambda e: e.iota(o, pattern, base, cm, allow_small_or_imprecise_dtypes=True), [], w)
+        else:
+            op("g", lambda e: e.iota(o, pattern, base, cm), [], w)
+
+    iota(T.qi[:, 0:4], [[0, 4]], 0, 1, ["qi"])
+    iota(T.uf[:, 0:4], [[2, 4]], 0, 0, ["ufa"], True)
+    iota(T.uf[:, 4:8], [[32, 4]], 96, 0, ["ufb"], True)
+    iota(T.ui[:, 0:48], [[-16, 6], [32, 4], [0, 2]], 97, 0, ["ui"])
+    iota(T.w4[:], [[4, 320]], 1280, 0, ["w4"], True)
+    iota(T.jj[:], [[1, 320]], 128, -1, ["jj"])
+    iota(T.jk[:], [[1, 320]], 0, 0, ["jk"])
+    for a in range(4):
+        iota(T.cid[32 * a:32 * a + 32, 0:10], [[128, 10]], 1280, 4, ["cid%d" % a], True)
+    CID = ["cid%d" % a for a in range(4)]
+    iota(T.cli[:, 0:10], [[1, 10]], 0, 0, ["cl16"])
+    iota(T.cli[:, 32:52], [[1, 10], [0, 2]], 0, 0, ["cl32"])
+
+    ts(T.qi[:, 4:8], T.qi[:, 0:4], 15, None, OP.bitwise_and, None, ["qi"], ["qa"])
+    q4 = T.qf[:, 0:4]
+    cp(q4, T.qi[:, 4:8], ["qa"], ["q4"])
+    tt(T.qf[:, 4:8], q4, T.uf[:, 0:4], OP.is_lt, ["q4", "ufa"], ["q_m"])
+    ts(T.qf[:, 8:12], q4, -16.0, None, OP.mult, None, ["q4"], ["q_r"])
+    tt(T.qf[:, 8:12], T.qf[:, 8:12], T.uf[:, 4:8], OP.add, ["q_r", "ufb"], ["q_r"])
+    lin(T.qf[:, 12:16], q4, 16, 16, ["q4"], ["q_l"])
+    tt(T.qf[:, 12:16], T.qf[:, 12:16], T.qf[:, 8:12], OP.subtract, ["q_l", "q_r"], ["q_l"])
+    tt(T.qf[:, 12:16], T.qf[:, 12:16], T.qf[:, 4:8], OP.mult, ["q_l", "q_m"], ["q_l"])
+    tt(T.qf[:, 8:12], T.qf[:, 8:12], T.qf[:, 12:16], OP.add, ["q_r", "q_l"], ["q_r"])
+    ts(T.qf[:, 16:20], q4, 6.0, None, OP.is_lt, None, ["q4"], ["q_6"])
+    tt(T.qf[:, 8:12], T.qf[:, 8:12], T.qf[:, 16:20], OP.mult, ["q_r", "q_6"], ["q_r"])
+    for k, (c, spec) in enumerate(((4, ((7, 112.0), (8, 1.0), (9, 113.0))), (1, ((6, 112.0), (8, 113.0), (9, 1.0))))):
+        o = 32 + 32 * k
+        for j, (q, val) in enumerate(spec):
+            ts(T.qf[:, o + 4 * j:o + 4 * j + c], T.qf[:, 0:c], float(q), val, OP.is_equal, OP.mult, ["q4"], ["qs%d%d" % (k, j)])
+        tt(T.qf[:, o:o + c], T.qf[:, o:o + c], T.qf[:, o + 4:o + 4 + c], OP.add, ["qs%d0" % k, "qs%d1" % k], ["qs%d0" % k])
+        tt(T.qf[:, o:o + c], T.qf[:, o:o + c], T.qf[:, o + 8:o + 8 + c], OP.add, ["qs%d0" % k, "qs%d2" % k], ["qs%d0" % k])
+    cp(T.qf[:, 32:33], T.qf[:, 64:65], ["qs10", "qs00"], ["qs00"])
+    tt(T.qf[:, 8:12], T.qf[:, 8:12], T.qf[:, 32:36], OP.add, ["q_r", "qs00"], ["q_r"])
+    cp(T.uoff[:, 0:8:2], T.qf[:, 8:12], ["q_r"], ["uoff0"])
+    cp(T.uoff[:, 1:8:2], T.qf[:, 8:12], ["q_r"], ["uoff1"])
+    quant(T.uq[:, 0:128], T.us[:, 0:128], T.ub[:, 0:512], ["ub"], ["uq"])
+    cp(T.utq[:, 0:128].bitcast(dt.uint32), T.uq[:, 0:128].bitcast(dt.uint32).indirect(T.uoff[:, 0:8]), ["uq", "uoff0", "uoff1"], ["utq"])
+    cp(T.uts[:, 0:128], T.us[:, 0:128].indirect(T.uoff[:, 0:8]), ["uq", "uoff0", "uoff1"], ["uts"], "a")
+
+    ts(T.jj[:], T.jj[:], 15, None, OP.bitwise_and, None, ["jj"], ["jj"])
+    ts(T.mask[:], T.jj[:], 0.0, None, OP.is_equal, None, ["jj"], ["mask"])
+    ts(T.jk[:], T.jk[:], 15, None, OP.bitwise_and, None, ["jk"], ["jk"])
+    ts(T.rs[:], T.jk[:], 0.0, BIG, OP.is_gt, OP.mult, ["jk"], ["rs"])
+
+    def list_of(s):
+        cp(T.nlu[:, 40 * s:40 * s + 40], T.nl[:, 40 * s:40 * s + 40], ["nl%d" % s], ["nlu%d" % s])
+
+    def window(s, q):
+        cp(T.tw[:, 640 * s:640 * s + 640], T.w4[:].indirect(T.nlu[:, 40 * s:40 * s + 40]), ["w4", "nlu%d" % s], ["tw%d" % s], q)
+
+    for s in (6, 0, 7, 1):
+        list_of(s)
+    window(0, "a")
+    window(6, "v")
+    window(1, "a")
+    for h in (0, 1):
+        quant(T.qx0[:, 160 * h:160 * h + 160], T.sx0[:, 160 * h:160 * h + 160], T.x0[:, 640 * h:640 * h + 640], ["x0%d" % h], ["qx0%d" % h])
+    for s in (2, 3, 4, 5):
+        list_of(s)
+    window(2, "a")
+    for k in range(3):
+        w = 320 if k < 2 else 160
+        cp(T.rb[:, 320 * k:320 * k + w], T.rs[:, 0:w], ["rs"], ["rb%d" % s for s in ((1, 2), (3, 4), (5,))[k]])
+    cp(T.clu[:, 0:10], T.cli[:, 0:10], ["cl16"], ["c16"])
+    cp(T.clu[:, 32:52], T.cli[:, 32:52], ["cl32"], ["c32"])
+    cp(T.lt0[0:32, 0:10], T.cid[0:32, 0:10], CID, ["lt0_0"])
+    ts(T.mlu[96:128, 1:20:2], T.cid[96:128, 0:10], 0.25, None, OP.mult, None, CID, ["ml_o3"])
+    fill(T.ones[:], 1.0, ["ones"])
+    for b in range(4):
+        op("g", lambda e: e.affine_select(T.et[:, 512 * b:512 * b + 512], T.ones[:], [[1, 512]], OP.is_equal, 0.0, -b, -4), ["ones"], ["et%d" % b])
+
+    def half_x(k, h):
+        x = T["x%d" % k]
+        for n in ("xh", "xg"):
+            op("a", lambda e: e.activation(T[n][:, 640 * h:640 * h + 640], x[:, 640 * h:640 * h + 640], AF.Copy, scale=0.5), ["x%d%d" % (k, h)], ["%s%d" % (n, h)])
+
+    window(3, "a")
+    half_x(0, 0)
+    half_x(0, 1)
+    window(4, "a")
+    window(5, "a")
+
+    def scores(k, h):
+        mm(h, 160, T.utq[:], T.uts[:], T["qx%d" % k][:, 160 * h:160 * h + 160], T["sx%d" % k][:, 160 * h:160 * h + 160], ["utq", "uts", "qx%d%d" % (k, h)])
+        tr(T.st[:, 160 * h:160 * h + 160], bank(h, 160), ["b%d" % h], ["st%d" % h])
+
+    ST = ["st0", "st1"]
+
+    def row(q):
+        return T.st[:, q:320:32]
+
+    def tmp(k):
+        return T.tmp[:, 16 * k:16 * k + 10]
+
+    def rstart(s):
+        return T.rb[:, 160 * (s - 1):160 * s:16]
+
+    def flips(k, first):
+        qx, sx = T["qx%d" % k], T["sx%d" % k]
+        for s in range(6):
+            mm(2 + s, 320, T.ufq[:, 128 * s:128 * s + 128], T.ufs[:, 128 * s:128 * s + 128], qx[:], sx[:], ["ufq", "ufs", "qx%d0" % k, "qx%d1" % k])
+        for s in range(6):
+            if first:
+                for j, sg in ((0, T.sgn), (1, T.sgc)):
+                    o = T.nw[:, 640 * s + 320 * j:640 * s + 320 * j + 320]
+                    op("a", lambda e: e.activation(o, bank(2 + s, 320), AF.Sign, bias=EPS if j else -EPS, scale=sg[:, s:s + 1]), ["b%d" % (2 + s), "sgc"], ["nw%d%d" % (s, j)])
+            else:
+                op("a", lambda e: e.activation(T.sg2[:, 320 * s:320 * s + 320], bank(2 + s, 320), AF.Sign, bias=EPS, scale=T.sgc[:, s:s + 1]), ["b%d" % (2 + s), "sgc"], ["sg2%d" % s])
+
+    def both(s):
+        p = T.nw[:, 640 * s + 320:640 * s + 640]
+        tt(p, p, T.sg2[:, 320 * s:320 * s + 320], OP.mult, ["nw%d1" % s, "sg2%d" % s], ["nw%d1" % s])
+        op("a", lambda e: e.activation(T.nw[:, 640 * s:640 * s + 320], p, AF.Copy, scale=-1.0), ["nw%d1" % s], ["nw%d0" % s])
+
+    def direct(n, rd):
+        dv = (T.dva, T.dvb)[n][:, 0:10]
+        name = ("dva", "dvb")[n]
+        o = 5 * n
+        if rd == 1:
+            ts(tmp(o), row(6 + n), 0.0, 2.0, OP.is_gt, OP.mult, ST, ["t%d" % o])
+            tt(tmp(o), tmp(o), T.cid[:, 0:10], OP.add, ["t%d" % o] + CID, ["t%d" % o])
+            lin(T.nu[:, 96 + 16 * n:106 + 16 * n], tmp(o), 0.5, -640, ["t%d" % o], ["nu%d" % (6 + n)])
+            tt(T.ye[:, 160 * n:160 * n + 160], T.tw[:, 640 * (6 + n):640 * (7 + n)].indirect(T.nu[:, 96 + 16 * n:106 + 16 * n]), mask1, OP.mult,
+               ["tw%d" % (6 + n), "nu%d" % (6 + n), "mask"], ["ye%d" % n])
+            scan(T.yes[:, 160 * n:160 * n + 160], rst1, T.ye[:, 160 * n:160 * n + 160], OP.min, OP.add, ["rs", "ye%d" % n], ["yes%d" % n])
+            cp(dv, T.yes[:, 160 * n + 15:160 * n + 160:16], ["yes%d" % n], [name])
+        else:
+            e, d = (T.ea, T.eb)[n][:, 0:10], (T.da, T.db)[n][:, 0:10]
+            ts(tmp(o), row(6 + n), 0.0, None, OP.is_gt, None, ST, ["t%d" % o])
+            ts(tmp(o + 1), row(8 + n), T.sgc[:, 6 + n:7 + n], 0.0, OP.mult, OP.is_lt, ST + ["sgc"], ["t%d" % (o + 1)])
+            tt(tmp(o + 2), tmp(o), tmp(o + 1), OP.not_equal, ["t%d" % o, "t%d" % (o + 1)], ["t%d" % (o + 2)])
+            tt(tmp(o + 2), tmp(o + 2), d, OP.mult, ["t%d" % (o + 2), "d%d" % n], ["t%d" % (o + 2)])
+            tt(dv, e, tmp(o + 2), OP.add, ["e%d" % n, "t%d" % (o + 2)], [name])
+
+    def turn_direct(n):
+        o = 5 * n
+        e, d = (T.ea, T.eb)[n][:, 0:10], (T.da, T.db)[n][:, 0:10]
+        tt(tmp(o + 3), tmp(o + 1), d, OP.mult, ["t%d" % (o + 1), "d%d" % n], ["t%d" % (o + 3)])
+        tt(e, e, tmp(o + 3), OP.add, ["e%d" % n, "t%d" % (o + 3)], ["e%d" % n])
+        tt(d, d, tmp(o + 3), OP.subtract, ["d%d" % n, "t%d" % (o + 3)], ["d%d" % n])
+        tt(d, d, tmp(o + 3), OP.subtract, ["d%d" % n, "t%d" % (o + 3)], ["d%d" % n])
+
+    def lu(s):
+        return T.lu[:, 16 * s:16 * s + 10]
+
+    def walk(rd):
+        fl = rd > 1
+        rsc, cm, cb = (1280.0, 0.25, -320) if fl else (2.0, 0.5, -640)
+
+        def bits(s):
+            ts(rstart(s), row(s), 0.0, rsc, OP.is_gt, OP.mult, ST, ["rb%d" % s])
+
+        direct(0, rd)
+        ts(tmp(10), row(0), 0.0, rsc, OP.is_gt, OP.mult, ST, ["t10"])
+        tt(tmp(10), tmp(10), T.dva[:, 0:10], OP.add, ["t10", "dva"], ["t10"])
+        lin(lu(0), tmp(10), cm, cb, ["t10"], ["lu0a"])
+        if fl:
+            tt(T.y2i[:], T.dva[:, 0:10].indirect(T.clu[:, 0:10]), mask1, OP.mult, ["dva", "c16", "mask"], ["y2i"])
+        if rd == 3:
+            both(0)
+            both(1)
+        for s in range(6):
+            L = ["lu%d%s" % (s, c) for c in "abc"]
+            if rd == 3 and s + 2 < 6:
+                both(s + 2)
+            prev = "y2i" if s == 0 else "y2%d" % (s - 1)
+            if fl:
+                pv = T.y2i[:] if s == 0 else T.y2[:, 160 * (s - 1):160 * s]
+                tt(T.y1[:], T.nw[:, 640 * s:640 * s + 640].indirect(lu(s)), pv, OP.add, L + ["nw%d0" % s, "nw%d1" % s, prev, prev + "x"], ["y1"])
+            if s < 5:
+                bits(s + 1)
+            if fl:
+                scan(T.y1s[:], rst1, T.y1[:], OP.min, OP.max, ["rs", "y1"], ["y1s"])
+                nu = T.nu[:, 16 * s:16 * s + 10]
+                lin(nu, T.y1s[:, 15:160:16], 0.5, -639.5, ["y1s"], ["nu%d" % s])
+                L, lst = ["nu%d" % s], nu
+            else:
+                lst = lu(s)
+            y2, y2s = T.y2[:, 160 * s:160 * s + 160], T.y2s[:, 160 * s:160 * s + 160]
+            tt(y2, T.tw[:, 640 * s:640 * s + 640].indirect(lst), mask1, OP.mult, L + ["tw%d" % s, "mask"], ["y2%d" % s, "y2%dx" % s])
+            rs = T.rb[:, 160 * s:160 * s + 160] if s < 5 else rst1
+            scan(y2s, rs, y2, OP.min, OP.add, ["y2%d" % s, "rb%d" % (s + 1), "rs"], ["y2s%d" % s])
+
+            def last(lo, hi):
+                return T.y2s[lo:hi, 160 * s + 15:160 * s + 160:16]
+
+            def rst(lo, hi):
+                return T.rb[lo:hi, 160 * s:160 * s + 160:16]
+
+            if s < 5:
+                n = 16 * (s + 1)
+                for k, (lo, hi) in enumerate({1: ((0, 32), (64, 128)), 3: ((0, 64), (96, 128))}.get(s, ((0, 128),))):
+                    lin(T.lu[lo:hi, n:n + 10], last(lo, hi), cm, cb, ["y2s%d" % s], ["lu%d%s" % (s + 1, "ab"[k])])
+            if s in (1, 3) and fl:
+                lo = 32 if s == 1 else 64
+                cp(T.y2[lo:lo + 32, 160 * s:160 * s + 160], T.y2b[lo:lo + 32, :], ["y2b", "y2%d" % s], ["y2%dx" % s])
+            lo = 32 * (1 + s // 2)
+            lt = (T.lt0, T.lt1)[s % 2]
+            if s < 5:
+                tt(lt[lo:lo + 32, 0:10], last(lo, lo + 32), rst(lo, lo + 32), OP.subtract, ["y2s%d" % s, "rb%d" % (s + 1)], ["lt%d_%d" % (s % 2, lo // 32)])
+            else:
+                cp(lt[lo:lo + 32, 0:10], last(lo, lo + 32), ["y2s5"], ["lt1_3"])
+            if s == 0:
+                direct(1, rd)
+                cp(T.lt1[0:32, 0:10], T.dvb[0:32, 0:10], ["dvb"], ["lt1_0"])
+                lin(T.mlu[96:128, 0:20:2], T.dvb[96:128, 0:10], 0.25, -320, ["dvb"], ["ml_e3"])
+                if fl:
+                    tt(T.y2b[:], T.dvb[:, 0:10].indirect(T.clu[:, 0:10]), mask1, OP.mult, ["dvb", "c16", "mask"], ["y2b"])
+            if s in (0, 2):
+                k = s + 2
+                lo = 16 * k
+                if k == 2:
+                    ts(tmp(11), row(2), 0.0, rsc, OP.is_gt, OP.mult, ST, ["t11"])
+                else:
+                    ts(tmp(11), row(4), 0.0, rsc, OP.is_gt, OP.mult, ST, ["t11"])
+                tt(tmp(11), tmp(11), T.dvb[:, 0:10], OP.add, ["t11", "dvb"], ["t11"])
+                lin(T.lu[lo:lo + 32, 16 * k:16 * k + 10], T.tmp[lo:lo + 32, 176:186], cm, cb, ["t11"], ["lu%dc" % k])
+            if s == 4:
+                tt(T.tmp[0:96, 192:202], last(0, 96), rst(0, 96), OP.subtract, ["y2s4", "rb5"], ["t12"])
+                ts(T.mlu[0:96, 1:20:2], T.tmp[0:96, 192:202], 0.25, None, OP.mult, None, ["t12"], ["ml_o"])
+                op("a", lambda e: e.activation(T.bc0[:], T.lt0[:, 0:10].indirect(T.clu[:, 32:52]), AF.Copy, bias=-480.0, scale=0.25),
+                   ["c32"] + ["lt0_%d" % a for a in range(4)], ["bc0"])
+            if s == 5:
+                op("v", lambda e: e.tensor_scalar(T.bc1[:], T.lt1[:, 0:10].indirect(T.clu[:, 32:52]), 0.25, -480.0, OP.mult, OP.add),
+                   ["c32"] + ["lt1_%d" % a for a in range(4)], ["bc1"])
+                lin(T.mlu[0:96, 0:20:2], last(0, 96), 0.25, -320, ["y2s5"], ["ml_e"])
+        tr(T.lw[:, 0:320], T.bc0[:], ["bc0"], ["lw0"])
+        tr(T.lw[:, 320:640], T.bc1[:], ["bc1"], ["lw1"])
+        cp(T.km[:], T.lw[:].indirect(T.mlu[:, 0:20]), ["lw0", "lw1", "ml_e", "ml_o", "ml_e3", "ml_o3"], ["km"])
+        tr(T.kt[:], T.km[:], ["km"], ["kt"])
+        for t in range(4):
+            lin(T.of[:, 32 * t:32 * t + 20], T.kt[:, 0:320:16], 4, 640 + t, ["kt"], ["of%d" % t])
+        lin(T["kl%d" % rd][:], T.kt[:, 0:320:16], 1, 160, ["kt"], ["kl%d" % rd])
+
+    sent = [0]
+
+    def send(rd, what, h):
+        dst = T.cores[rank ^ STEP[rd - 1]]
+        if what == "k":
+            need("g", deps_of(["kl%d" % rd], []))
+        else:
+            need("g", deps_of(["qh%d%d" % (rd, h)], []))
+        q, s, lq, ls = T["qh%d" % rd], T["sh%d" % rd], T["lq%d" % rd], T["ls%d" % rd]
+        if topo.may_write(core, dst):
+            rid, pid = topo.addr(dst, core)
+            m, n = topo.mask(core, dst), len(topo.engines(core, dst))
+            if what == "k":
+                g.remote_dma(T["kr%d" % rd][:], T["kl%d" % rd][:], T.sem["kr%d" % rd], T.sem.lsem, pid, rid, m)
+                sent[0] += n
+                wrote["kr%d" % rd] = ("kr%d" % rd, n)
+                return
+            a = 160 * h
+            sem = T.sem["ar%d%d" % (rd, h)]
+            g.remote_dma(lq[:, a:a + 160].bitcast(dt.uint8), q[:, a:a + 160].bitcast(dt.uint8), sem, T.sem.lsem, pid, rid, m)
+            g.remote_dma(ls[:, a:a + 160], s[:, a:a + 160], sem, T.sem.lsem, pid, rid, m)
+            sent[0] += 2 * n
+            wrote["lq%d%d" % (rd, h)] = ("ar%d%d" % (rd, h), 2 * n)
+            return
+        rel = relays_of(core, dst, topo)
+        ways = [topo.addr(k, core) for k in rel]
+        eng = topo.engines(core, rel[0])
+        n = len(eng) // 2
+        masks = [bits_of(eng[:n]), bits_of(eng[n:])]
+        far = len(topo.engines(rel[0], dst))
+        if what == "k":
+            g.remote_dma(T.rlk[:], T["kl%d" % rd][:], T.sem.rk, T.sem.lsem, ways[0][1], ways[0][0], masks[0])
+            sent[0] += n
+            wrote["kr%d" % rd] = ("kr%d" % rd, far)
+            return
+
+        def both_ways(view, land):
+            tr_ = []
+            for k in (0, 1):
+                a = 160 * h + 80 * k
+                tr_.append(RemoteDMATransfer(dst_ids=[DstId(rid=ways[k][0], pnc=ways[k][1])], dma_engine_mask=masks[k], remote_sem=T.sem["ry%d" % h],
+                                             src=view(a), dst=land(a)))
+            g.remote_dma_fused(tr_, local_sem=T.sem.lsem)
+            sent[0] += 2 * n
+
+        both_ways(lambda a: q[:, a:a + 80].bitcast(dt.uint8), lambda a: T.rlq[:, a:a + 80].bitcast(dt.uint8))
+        both_ways(lambda a: s[:, a:a + 80], lambda a: T.rls[:, a:a + 80])
+        wrote["lq%d%d" % (rd, h)] = ("ar%d%d" % (rd, h), 4 * far)
+
+    def meet(h):
+        for t in range(4):
+            tt(T.vt[:, 640 * h + t:640 * h + 640:4], T.xh[:].indirect(T.of[:, 32 * t + 10 * h:32 * t + 10 * h + 10]), T.xg[:, 640 * h + t:640 * h + 640:4], OP.add,
+               ["xh0", "xh1", "xg%d" % h, "of%d" % t], ["vt%d%d" % (h, t)])
+
+    def layer(h):
+        c = slice(160 * h, 160 * h + 160)
+        for b in range(4):
+            mm(4 * h + b, 160, T.wq[:, 128 * b:128 * b + 128], T.wsp[:, 128 * b:128 * b + 128], T.qv[:, c], T.qvs[:, c], ["wq", "qv%d" % h])
+
+    def layer_out(h, b, q):
+        o, i = T.ht[:, 640 * h + b:640 * h + 640:4], bank(4 * h + b, 160)
+        if q == "a":
+            op("a", lambda e: e.activation(o, i, AF.Copy, scale=0.03125), ["b%d" % (4 * h + b)], ["ht%d%d" % (h, b)])
+        else:
+            ts(o, i, 0.03125, None, OP.mult, None, ["b%d" % (4 * h + b)], ["ht%d%d" % (h, b)])
+
+    def quant_v(h):
+        quant(T.qv[:, 160 * h:160 * h + 160], T.qvs[:, 160 * h:160 * h + 160], T.vt[:, 640 * h:640 * h + 640], ["vt%d%d" % (h, t) for t in range(4)], ["qv%d" % h])
+
+    def quant_h(rd, h):
+        quant(T["qh%d" % rd][:, 160 * h:160 * h + 160], T["sh%d" % rd][:, 160 * h:160 * h + 160], T.ht[:, 640 * h:640 * h + 640],
+              ["ht%d%d" % (h, b) for b in range(4)], ["qh%d%d" % (rd, h)])
+
+    def natural(k, rd):
+        mm(0, 320, T.uq[:], T.us[:], T["qx%d" % k][:], T["sx%d" % k][:], ["uq", "qx%d0" % k, "qx%d1" % k])
+        cp(T.sn[:], bank(0, 320), ["b0"], ["sn"], "a")
+        dma("s", [(T.fn[:], T.sn[1:128:16, :])], ["sn"], ["fn"], "fn%d" % rd)
+
+    def turn_tables():
+        for k, (tab, f) in enumerate(((T.ltb, OP.is_lt), (T.rtb, OP.is_gt))):
+            n = "lr%d" % k
+            a, b = T.lt2[:, 32 * k:32 * k + 20], n + "t"
+            e0, e1 = tab[:, 0:40:2], tab[:, 1:40:2]
+            z = T.qf[:, 32 * k:32 * k + 20]
+            ts(a, T.fn[:], 0.0, None, f, None, ["fn"], [b])
+            tt(z, e1, e0, OP.subtract, [n], [n + "z"])
+            tt(z, z, a, OP.mult, [n + "z", b], [n + "z"])
+            tt(e0, e0, z, OP.add, [n, n + "z"], [n])
+            tt(e1, e1, z, OP.subtract, [n, n + "z"], [n])
+
+    for h in (0, 1):
+        scores(0, h)
+    window(7, "v")
+    for rd in (1, 2, 3):
+        walk(rd)
+        send(rd, "k", 0)
+        meet(0)
+        quant_v(0)
+        layer(0)
+        for b in range(4):
+            layer_out(0, b, "a")
+        meet(1)
+        quant_v(1)
+        layer(1)
+        quant_h(rd, 0)
+        send(rd, "h", 0)
+        for b in range(4):
+            layer_out(1, b, "av"[b % 2])
+        quant_h(rd, 1)
+        send(rd, "h", 1)
+        if rd == 1:
+            quant(T.eq[:], T.es[:], T.et[:], ["et%d" % b for b in range(4)], ["eq"])
+            for s in range(6):
+                fill(T.ui[:, 8 * s + 2 * (s // 2 + 1):8 * s + 8], 16 * (s + 1) + 1, ["ui"])
+            cp(T.uoff[:, 8:56], T.ui[:, 0:48], ["ui"], ["uoff2"])
+            fill(T.sgc[:], 1.0, ["sgc"])
+            for hi, lo in ((32, 0), (64, 2), (96, 4)):
+                fill(T.sgc[0:hi, lo:6], -1.0, ["sgc"])
+            fill(T.sgc[0:32, 6:7], -1.0, ["sgc"])
+            fill(T.sgc[32:64, 7:8], -1.0, ["sgc"])
+            fill(T.sgc[64:128, 7:8], -1.0, ["sgc"])
+            ts(T.sgn[:], T.sgc[:], -1.0, None, OP.mult, None, ["sgc"], ["sgc"])
+            cp(T.ufq[:].bitcast(dt.uint32), T.uq[:, 0:128].bitcast(dt.uint32).indirect(T.uoff[:, 8:56]), ["uq", "uoff2"], ["ufq"])
+            cp(T.ufs[:], T.us[:, 0:128].indirect(T.uoff[:, 8:56]), ["uq", "uoff2"], ["ufs"], "a")
+            for n in (0, 1):
+                for c in (0, 1):
+                    k = 2 * n + c
+                    if n == 0:
+                        lin(T.lu[:, 96 + 16 * c:106 + 16 * c], T.cid[:, 0:10], 0.5, -640 + c, CID, ["lc%d" % c])
+                    tt(T.ye[:, 160 * k:160 * k + 160], T.tw[:, 640 * (6 + n):640 * (7 + n)].indirect(T.lu[:, 96 + 16 * c:106 + 16 * c]), mask1, OP.mult,
+                       ["tw%d" % (6 + n), "lc%d" % c, "mask"], ["ye%d" % k])
+                    scan(T.yes[:, 160 * k:160 * k + 160], rst1, T.ye[:, 160 * k:160 * k + 160], OP.min, OP.add, ["rs", "ye%d" % k], ["yes%d" % k])
+                e, d = (T.ea, T.eb)[n][:, 0:10], (T.da, T.db)[n][:, 0:10]
+                first, second = T.yes[:, 320 * n + 15:320 * n + 160:16], T.yes[:, 320 * n + 175:320 * n + 320:16]
+                cp(e, first, ["yes%d" % (2 * n)], ["e%d" % n])
+                tt(d, second, first, OP.subtract, ["yes%d" % (2 * n), "yes%d" % (2 * n + 1)], ["d%d" % n])
+            cp(T.lnu[:], T.lni[:], ["lni"], ["lnu"])
+        else:
+            natural(rd - 1, rd - 1)
+            if rd == 2:
+                turn_direct(0)
+                turn_direct(1)
+            turn_tables()
+        kl, kr = T["kl%d" % rd], T["kr%d" % rd]
+        cp(T.kw[:], T.w4[:].indirect(kr[:]), ["w4", "kr%d" % rd], ["kw"], "a")
+        tt(T.ky[:], T.kw[:].indirect(kl[:]), T.mask[:], OP.mult, ["kw", "kl%d" % rd, "mask"], ["ky"])
+        scan(T.kys[:], T.rs[:], T.ky[:], OP.min, OP.add, ["ky", "rs"], ["kys"])
+        for t in range(4):
+            lin(T.mo[:, 32 * t:32 * t + 20], T.kys[:, 15:320:16], 1, -1280 + t, ["kys"], ["mo%d" % t])
+        if rd == 1:
+            for k, tgt in ((0, T.lrow), (1, T.rrow)):
+                cp(tgt[:], T.w4[:].indirect(T.lnu[:, 40 * k:40 * k + 40]), ["w4", "lnu"], ["row%d" % k], "a")
+                dma("s", [((T.ltb, T.rtb)[k][:], tgt[0:128:16, :])], ["row%d" % k], ["lr%d" % k], "dt%d" % k)
+        if rd == 3:
+            quant(T.vq[:], T.vs[:], T.vb[:], ["vb"], ["vq"])
+        for h in (0, 1):
+            lq, ls = T["lq%d" % rd], T["ls%d" % rd]
+            for b in range(4):
+                mm(4 * h + b, 160, T.eq[:, 128 * b:128 * b + 128], T.es[:, 128 * b:128 * b + 128], lq[:, 160 * h:160 * h + 160], ls[:, 160 * h:160 * h + 160],
+                   ["eq", "lq%d%d" % (rd, h)])
+            for b in range(4):
+                cp(T.dd[:, 640 * h + b:640 * h + 640:4], bank(4 * h + b, 160), ["b%d" % (4 * h + b)], ["dd%d%d" % (h, b)], "av"[b % 2])
+        xn, qn, sn = T["x%d" % rd], T["qx%d" % rd], T["sx%d" % rd]
+        for h in (0, 1):
+            for t in range(4):
+                tt(xn[:, 640 * h + t:640 * h + 640:4], T.dd[:].indirect(T.mo[:, 32 * t + 10 * h:32 * t + 10 * h + 10]), T.vt[:, 640 * h + t:640 * h + 640:4], OP.add,
+                   ["mo%d" % t, "vt%d%d" % (h, t)] + ["dd%d%d" % (i, b) for i in (0, 1) for b in range(4)], ["x%d%d" % (rd, h), "xn%d%d%d" % (rd, h, t)])
+            quant(qn[:, 160 * h:160 * h + 160], sn[:, 160 * h:160 * h + 160], xn[:, 640 * h:640 * h + 640], ["x%d%d" % (rd, h)] + ["xn%d%d%d" % (rd, h, t) for t in range(4)], ["qx%d%d" % (rd, h)])
+            if rd == 3:
+                c = slice(160 * h, 160 * h + 160)
+                dma("s", [(T.oc[:, 640 * h:640 * h + 640], qn[:, c].bitcast(dt.uint8))] + [(T.osc[4 * k:4 * k + 4, c], sn[32 * k:32 * k + 4, c]) for k in range(4)],
+                    ["qx3%d" % h], [], "oq%d" % h)
+            else:
+                scores(rd, h)
+        if rd < 3:
+            flips(rd, rd == 1)
+            half_x(rd, 0)
+            half_x(rd, 1)
+    natural(3, 3)
+    mm(1, 320, T.vq[:], T.vs[:], T.qx3[:], T.sx3[:], ["vq", "qx30", "qx31"])
+    cp(T.yb[:], bank(1, 320), ["b1"], ["yb"])
+    dma("s", [(T.y[:], T.yb[:])], ["yb"], [], "oy")
+    turn_tables()
+    for k, tab in enumerate((T.ltb, T.rtb)):
+        lin(T.lout[:, 40 * k:40 * k + 40], tab[:], 0.25, -320, ["lr%d" % k], ["lo%d" % k])
+        dma("s", [(T.lr[:, 640 * k:640 * k + 640], T.lout[:, 40 * k:40 * k + 40])], ["lo%d" % k], [], "ol")
+    need("g", dict(total))
+    g.wait_ge(T.sem.lsem, sent[0])
+    for rd in (1, 2, 3):
+        for k in ("kr%d" % rd, "lq%d0" % rd, "lq%d1" % rd):
+            need("g", {wrote[k][0]: wrote[k][1]})

@@ -6,6 +6,7 @@ OP = AluOpType
 AF = ActivationFunctionType
 STEP = [4, 1, 2]
 BIG = 1.0e6
+WAKE, SPARE, LOOK = 0.07, 0.5, 0.3
 EPS = 2.0 ** -93
 
 F, B, I, U, C4, S8 = "float32", "bfloat16", "int32", "uint16", "float8_e4m3fn_x4", "uint8"
@@ -19,7 +20,8 @@ for _n, _w, _d in [
     ("qv", 320, C4), ("qvs", 320, S8),
     ("qh1", 320, C4), ("sh1", 320, S8), ("qh2", 320, C4), ("sh2", 320, S8), ("qh3", 320, C4), ("sh3", 320, S8),
     ("lq1", 320, C4), ("ls1", 320, S8), ("lq2", 320, C4), ("ls2", 320, S8), ("lq3", 320, C4), ("ls3", 320, S8), ("rlq", 320, C4), ("rls", 320, S8),
-    ("nl", 320, I), ("nlu", 320, U), ("tw", 5120, F), ("nw", 3840, B), ("sg2", 1920, B), ("w4", 320, F),
+    ("nl", 320, I), ("nlu", 320, U), ("tw", 5120, F), ("tx", 3840, F), ("nw", 3840, B), ("w4", 320, F),
+    ("cw", 120, F), ("cx", 120, F), ("fb", 60, F), ("fx", 120, F), ("fl", 240, F), ("flu", 256, U), ("lz", 64, F),
     ("jj", 320, I), ("jk", 320, I), ("mask", 320, F), ("rs", 320, F), ("rb", 800, F), ("st", 320, F),
     ("cid", 16, F), ("dva", 16, F), ("dvb", 16, F), ("ea", 16, F), ("da", 16, F), ("eb", 16, F), ("db", 16, F), ("tmp", 256, F),
     ("y1", 160, F), ("y1s", 160, F), ("y2i", 160, F), ("y2b", 160, F), ("y2", 960, F), ("y2s", 960, F), ("ye", 640, F), ("yes", 640, F),
@@ -31,7 +33,7 @@ for _n, _w, _d in [
 ]:
     SCRATCH[_n] = ("sbuf", [128, _w], _d)
 
-SEMAPHORES = (["sv", "sa", "st", "sg", "dx0", "dx1", "du", "dv", "dw", "dl", "dt0", "dt1", "fn1", "fn2", "fn3", "oy", "ol", "oq0", "oq1", "lsem", "ry0", "ry1", "rk"]
+SEMAPHORES = (["sv", "sa", "st", "sg", "dx0", "dx1", "du", "dv", "dw", "dl", "dt0", "dt1", "fn1", "fn2", "fn3", "oy", "ol", "oq0", "oq1", "dfx", "lsem", "ry0", "ry1", "rk"]
               + ["dn%d" % s for s in range(8)] + ["ar%d%d" % (r, h) for r in (1, 2, 3) for h in (0, 1)] + ["kr%d" % r for r in (1, 2, 3)])
 
 
@@ -86,7 +88,118 @@ def rank_program(g, core, T, topo):
         return
     Q = {"g": g, "v": g.vector, "a": g.scalar, "t": g.tensor, "s": g.sync}
     SEM = {"g": "sg", "v": "sv", "a": "sa", "t": "st"}
-    total, waited, wrote, reads = {}, {}, {}, {}
+    nodes, writer, readers = [], {}, {}
+
+    def node(fns, cost, late, r, w, sem, inc):
+        pre, after = set(), set()
+        for k in list(r) + list(w):
+            if k in writer:
+                (after if k[0] == "@" else pre).add(writer[k])
+        for k in w:
+            if k[0] != "@":
+                pre.update(readers.get(k, ()))
+        i = len(nodes)
+        nodes.append({"fns": fns, "cost": cost, "late": late, "pre": sorted(pre), "order": sorted(pre | after), "sem": sem, "inc": inc})
+        for k in r:
+            readers.setdefault(k, set()).add(i)
+        for k in w:
+            writer[k] = i
+            readers[k] = set()
+
+    def op(q, fn, r, w, us):
+        node({q: fn}, {q: us}, 0.0, r, list(w) + (["gpsimd"] if q == "g" else []), None, 1)
+
+    def dma(q, pairs, r, w, sem):
+        def go(e):
+            for o, i in pairs:
+                e.dma_start(o, i).then_inc(T.sem[sem], 16)
+        node({q: go}, {q: 0.06 * len(pairs)}, 2.0, r, w, sem, 16 * len(pairs))
+
+    def us(n, cycles, gather):
+        return 0.05 + n * 0.0015 if gather else max(64, n * cycles) * 0.001
+
+    def tt(o, a, b, f, r, w, n=10, x=False, c=2):
+        op("v", lambda e: e.tensor_tensor(o, a, b, f), r, w, us(n, c, x))
+
+    def ts(o, a, s1, s2, f1, f2, r, w, n=10, x=False, c=1):
+        if f2 is None:
+            op("v", lambda e: e.tensor_scalar(o, a, s1, None, f1), r, w, us(n, c, x))
+        else:
+            op("v", lambda e: e.tensor_scalar(o, a, s1, s2, f1, f2), r, w, us(n, c, x))
+
+    def lin(o, a, m, b, r, w, n=10, x=False):
+        ts(o, a, float(m), float(b), OP.mult, OP.add, r, w, n, x)
+
+    def cp(o, a, r, w, q="v", n=10, x=False, c=1):
+        fns = {"v": lambda e: e.tensor_copy(o, a), "a": lambda e: e.activation(o, a, AF.Copy)}
+        node({k: fns[k] for k in q}, {k: us(n, c if k == "v" else 1, x) for k in q}, 0.0, r, w, None, 1)
+
+    def scaled(o, a, m, r, w, q, n, c=1):
+        fns = {"v": lambda e: e.tensor_scalar(o, a, m, None, OP.mult), "a": lambda e: e.activation(o, a, AF.Copy, scale=m)}
+        node({k: fns[k] for k in q}, {k: us(n, c if k == "v" else 1, False) for k in q}, 0.0, r, w, None, 1)
+
+    def tr(o, a, r, w, n, c=1):
+        op("v", lambda e: e.transpose(o, a), r, w, us(n, c, False))
+
+    def scan(o, d0, d1, f0, f1, r, w, n=160):
+        op("v", lambda e: e.tensor_tensor_scan(o, d0, d1, BIG, f0, f1), r, w, us(n, 1, False))
+
+    def mm(bank, n, lq, lsc, rq, rsc, r):
+        op("t", lambda e: e.matmul_mx(T.ps[:, 512 * bank:512 * bank + n], lq, lsc, rq, rsc, True, True), r, ["b%d" % bank], (n + 16) * 0.0011)
+
+    def fill(o, c, w, n=10):
+        op("v", lambda e: e.memset(o, c), [], w, us(n, 1, False))
+
+    def quant(q, s, t, r, w, n=640):
+        op("v", lambda e: e.quantize_mx(q, s, t), r, w, 0.012 + n * 0.00028)
+
+    def arrange():
+        n = len(nodes)
+        tail = [0.0] * n
+        out = [[] for _ in range(n)]
+        for i, d in enumerate(nodes):
+            for p in d["order"]:
+                out[p].append(i)
+        for i in range(n - 1, -1, -1):
+            d = nodes[i]
+            tail[i] = min(d["cost"].values()) + d["late"] + max([tail[k] + WAKE for k in out[i]] + [0.0])
+        left = [len(d["order"]) for d in nodes]
+        ready = [0.0] * n
+        open_ = [i for i in range(n) if left[i] == 0]
+        free, order = {}, []
+        while open_:
+            cand = []
+            for i in open_:
+                d = nodes[i]
+                for q in d["cost"]:
+                    s = max(free.get(q, 0.0), ready[i])
+                    extra = SPARE if q == "v" and len(d["cost"]) > 1 else 0.0
+                    cand.append((s, i, q, extra))
+            best = {}
+            for s, i, q, extra in cand:
+                e = s + nodes[i]["cost"][q] + extra
+                if i not in best or e < best[i][0]:
+                    best[i] = (e, s, q)
+            s0, i0 = min((v[1], i) for i, v in best.items())
+            q0 = best[i0][2]
+            same = [(i, v[1]) for i, v in best.items() if v[2] == q0]
+            i = max([k for k in same if k[1] <= s0 + 1e-9], key=lambda k: tail[k[0]])[0]
+            c = nodes[i]["cost"][q0]
+            soon = [k for k in same if k[1] < s0 + LOOK * c and tail[k[0]] > tail[i]]
+            if soon:
+                i = max(soon, key=lambda k: tail[k[0]])[0]
+            e, s, q = best[i]
+            open_.remove(i)
+            free[q] = s + nodes[i]["cost"][q]
+            order.append((s, len(order), i, q))
+            for k in out[i]:
+                left[k] -= 1
+                ready[k] = max(ready[k], free[q] + nodes[i]["late"] + WAKE)
+                if left[k] == 0:
+                    open_.append(k)
+        return [(i, q) for s, m, i, q in order]
+
+    total, waited = {}, {}
 
     def need(q, deps):
         for sem in sorted(deps):
@@ -94,71 +207,21 @@ def rank_program(g, core, T, topo):
                 waited[(q, sem)] = deps[sem]
                 Q[q].wait_ge(T.sem[sem], deps[sem])
 
-    def deps_of(r, w):
-        d = {}
-        for k in list(r) + list(w):
-            if k in wrote:
-                d[wrote[k][0]] = max(d.get(wrote[k][0], 0), wrote[k][1])
-        for k in w:
-            for sem, v in reads.get(k, {}).items():
-                d[sem] = max(d.get(sem, 0), v)
-        return d
-
-    def note(sem, r, w):
-        for k in r:
-            reads.setdefault(k, {})[sem] = total[sem]
-        for k in w:
-            wrote[k] = (sem, total[sem])
-            reads[k] = {}
-
-    def op(q, fn, r, w):
-        need(q, deps_of(r, w))
-        sem = SEM[q]
-        if q == "g" and total.get(sem, 0):
-            need(q, {sem: total[sem]})
-        fn(Q[q]).then_inc(T.sem[sem], 1)
-        total[sem] = total.get(sem, 0) + 1
-        note(sem, r, w)
-
-    def dma(q, pairs, r, w, sem):
-        need(q, deps_of(r, w))
-        for o, i in pairs:
-            Q[q].dma_start(o, i).then_inc(T.sem[sem], 16)
-            total[sem] = total.get(sem, 0) + 16
-        note(sem, r, w)
-
-    def tt(o, a, b, f, r, w):
-        op("v", lambda e: e.tensor_tensor(o, a, b, f), r, w)
-
-    def ts(o, a, s1, s2, f1, f2, r, w):
-        if f2 is None:
-            op("v", lambda e: e.tensor_scalar(o, a, s1, None, f1), r, w)
-        else:
-            op("v", lambda e: e.tensor_scalar(o, a, s1, s2, f1, f2), r, w)
-
-    def lin(o, a, m, b, r, w):
-        ts(o, a, float(m), float(b), OP.mult, OP.add, r, w)
-
-    def cp(o, a, r, w, q="v"):
-        if q == "v":
-            op("v", lambda e: e.tensor_copy(o, a), r, w)
-        else:
-            op("a", lambda e: e.activation(o, a, AF.Copy), r, w)
-
-    def tr(o, a, r, w):
-        op("v", lambda e: e.transpose(o, a), r, w)
-
-    def scan(o, d0, d1, f0, f1, r, w):
-        op("v", lambda e: e.tensor_tensor_scan(o, d0, d1, BIG, f0, f1), r, w)
-
-    def mm(bank, n, lq, lsc, rq, rsc, r):
-        op("t", lambda e: e.matmul_mx(T.ps[:, 512 * bank:512 * bank + n], lq, lsc, rq, rsc, True, True), r, ["b%d" % bank])
-
-    def fill(o, c, w):
-        op("v", lambda e: e.memset(o, c), [], w)
-
-    def quant(q, s, t, r, w):
-        op("v", lambda e: e.quantize_mx(q, s, t), r, w)
+    def issue():
+        done = {}
+        for i, q in arrange():
+            d = nodes[i]
+            deps = {}
+            for p in d["pre"]:
+                sem, v = done[p]
+                deps[sem] = max(deps.get(sem, 0), v)
+            need(q, deps)
+            inst = d["fns"][q](Q[q])
+            sem = d["sem"] or SEM[q]
+            if d["sem"] is None:
+                inst.then_inc(T.sem[sem], 1)
+            total[sem] = total.get(sem, 0) + d["inc"]
+            done[i] = (sem, total[sem])
 
     def bank(b, n):
         return T.ps[:, 512 * b:512 * b + n]
@@ -182,10 +245,13 @@ def rank_program(g, core, T, topo):
     dma("s", [(T.vb[:], T.v[:])], [], ["vb"], "dv")
 
     def iota(o, pattern, base, cm, w, fl=False):
+        n = 1
+        for step, count in pattern:
+            n *= count
         if fl:
-            op("g", lambda e: e.iota(o, pattern, base, cm, allow_small_or_imprecise_dtypes=True), [], w)
+            op("g", lambda e: e.iota(o, pattern, base, cm, allow_small_or_imprecise_dtypes=True), [], w, 0.15 + 0.002 * n)
         else:
-            op("g", lambda e: e.iota(o, pattern, base, cm), [], w)
+            op("g", lambda e: e.iota(o, pattern, base, cm), [], w, 0.15 + 0.002 * n)
 
     iota(T.qi[:, 0:4], [[0, 4]], 0, 1, ["qi"])
     iota(T.uf[:, 0:4], [[2, 4]], 0, 0, ["ufa"], True)
@@ -203,15 +269,20 @@ def rank_program(g, core, T, topo):
     ts(T.qi[:, 4:8], T.qi[:, 0:4], 15, None, OP.bitwise_and, None, ["qi"], ["qa"])
     q4 = T.qf[:, 0:4]
     cp(q4, T.qi[:, 4:8], ["qa"], ["q4"])
-    tt(T.qf[:, 4:8], q4, T.uf[:, 0:4], OP.is_lt, ["q4", "ufa"], ["q_m"])
-    ts(T.qf[:, 8:12], q4, -16.0, None, OP.mult, None, ["q4"], ["q_r"])
+    qe = T.qf[:, 20:24]
+    ts(T.qf[:, 24:28], q4, 10.0, -10.0, OP.is_ge, OP.mult, ["q4"], ["q_t"])
+    tt(qe, q4, T.qf[:, 24:28], OP.add, ["q4", "q_t"], ["qe"])
+    tt(T.qf[:, 4:8], qe, T.uf[:, 0:4], OP.is_lt, ["qe", "ufa"], ["q_m"])
+    ts(T.qf[:, 8:12], qe, -16.0, None, OP.mult, None, ["qe"], ["q_r"])
     tt(T.qf[:, 8:12], T.qf[:, 8:12], T.uf[:, 4:8], OP.add, ["q_r", "ufb"], ["q_r"])
-    lin(T.qf[:, 12:16], q4, 16, 16, ["q4"], ["q_l"])
+    lin(T.qf[:, 12:16], qe, 16, 16, ["qe"], ["q_l"])
     tt(T.qf[:, 12:16], T.qf[:, 12:16], T.qf[:, 8:12], OP.subtract, ["q_l", "q_r"], ["q_l"])
     tt(T.qf[:, 12:16], T.qf[:, 12:16], T.qf[:, 4:8], OP.mult, ["q_l", "q_m"], ["q_l"])
     tt(T.qf[:, 8:12], T.qf[:, 8:12], T.qf[:, 12:16], OP.add, ["q_r", "q_l"], ["q_r"])
-    ts(T.qf[:, 16:20], q4, 6.0, None, OP.is_lt, None, ["q4"], ["q_6"])
+    ts(T.qf[:, 16:20], qe, 6.0, None, OP.is_lt, None, ["qe"], ["q_6"])
     tt(T.qf[:, 8:12], T.qf[:, 8:12], T.qf[:, 16:20], OP.mult, ["q_r", "q_6"], ["q_r"])
+    ts(T.qf[:, 28:32], q4, 10.0, None, OP.is_ge, None, ["q4"], ["q_10"])
+    tt(T.qf[:, 8:12], T.qf[:, 8:12], T.qf[:, 28:32], OP.add, ["q_r", "q_10"], ["q_r"])
     for k, (c, spec) in enumerate(((4, ((7, 112.0), (8, 1.0), (9, 113.0))), (1, ((6, 112.0), (8, 113.0), (9, 1.0))))):
         o = 32 + 32 * k
         for j, (q, val) in enumerate(spec):
@@ -223,55 +294,57 @@ def rank_program(g, core, T, topo):
     cp(T.uoff[:, 0:8:2], T.qf[:, 8:12], ["q_r"], ["uoff0"])
     cp(T.uoff[:, 1:8:2], T.qf[:, 8:12], ["q_r"], ["uoff1"])
     quant(T.uq[:, 0:128], T.us[:, 0:128], T.ub[:, 0:512], ["ub"], ["uq"])
-    cp(T.utq[:, 0:128].bitcast(dt.uint32), T.uq[:, 0:128].bitcast(dt.uint32).indirect(T.uoff[:, 0:8]), ["uq", "uoff0", "uoff1"], ["utq"])
-    cp(T.uts[:, 0:128], T.us[:, 0:128].indirect(T.uoff[:, 0:8]), ["uq", "uoff0", "uoff1"], ["uts"], "a")
+    cp(T.utq[:, 0:128].bitcast(dt.uint32), T.uq[:, 0:128].bitcast(dt.uint32).indirect(T.uoff[:, 0:8]), ["uq", "uoff0", "uoff1"], ["utq"], n=128, x=True)
+    cp(T.uts[:, 0:128], T.us[:, 0:128].indirect(T.uoff[:, 0:8]), ["uq", "uoff0", "uoff1"], ["uts"], "av", n=128, x=True)
 
-    ts(T.jj[:], T.jj[:], 15, None, OP.bitwise_and, None, ["jj"], ["jj"])
-    ts(T.mask[:], T.jj[:], 0.0, None, OP.is_equal, None, ["jj"], ["mask"])
-    ts(T.jk[:], T.jk[:], 15, None, OP.bitwise_and, None, ["jk"], ["jk"])
-    ts(T.rs[:], T.jk[:], 0.0, BIG, OP.is_gt, OP.mult, ["jk"], ["rs"])
+    ts(T.jj[:], T.jj[:], 15, None, OP.bitwise_and, None, ["jj"], ["jj"], n=320)
+    ts(T.mask[:], T.jj[:], 0.0, None, OP.is_equal, None, ["jj"], ["mask"], n=320)
+    ts(T.jk[:], T.jk[:], 15, None, OP.bitwise_and, None, ["jk"], ["jk"], n=320)
+    ts(T.rs[:], T.jk[:], 0.0, BIG, OP.is_gt, OP.mult, ["jk"], ["rs"], n=320)
 
     def list_of(s):
         cp(T.nlu[:, 40 * s:40 * s + 40], T.nl[:, 40 * s:40 * s + 40], ["nl%d" % s], ["nlu%d" % s])
 
-    def window(s, q):
-        cp(T.tw[:, 640 * s:640 * s + 640], T.w4[:].indirect(T.nlu[:, 40 * s:40 * s + 40]), ["w4", "nlu%d" % s], ["tw%d" % s], q)
+    def window(s):
+        cp(T.tw[:, 640 * s:640 * s + 640], T.w4[:].indirect(T.nlu[:, 40 * s:40 * s + 40]), ["w4", "nlu%d" % s], ["tw%d" % s], "av", n=640, x=True)
 
-    for s in (6, 0, 7, 1):
+    for s in (6, 0, 7, 1, 2, 3, 4, 5):
         list_of(s)
-    window(0, "a")
-    window(6, "v")
-    window(1, "a")
+        window(s)
+    iota(T.cw[:], [[0, 6], [32, 20]], 0, 0, ["cw"], True)
+    ts(T.qf[:, 96:97], T.qf[:, 0:1], 2.0, None, OP.mult, None, ["q4"], ["q2"])
+    ts(T.cw[:], T.cw[:], T.qf[:, 96:97], None, OP.add, None, ["cw", "q2"], ["cw"], n=120)
+    lin(T.cx[:], T.cw[:], 1, 1, ["cw"], ["cx"], n=120)
     for h in (0, 1):
         quant(T.qx0[:, 160 * h:160 * h + 160], T.sx0[:, 160 * h:160 * h + 160], T.x0[:, 640 * h:640 * h + 640], ["x0%d" % h], ["qx0%d" % h])
-    for s in (2, 3, 4, 5):
-        list_of(s)
-    window(2, "a")
     for k in range(3):
         w = 320 if k < 2 else 160
-        cp(T.rb[:, 320 * k:320 * k + w], T.rs[:, 0:w], ["rs"], ["rb%d" % s for s in ((1, 2), (3, 4), (5,))[k]])
+        cp(T.rb[:, 320 * k:320 * k + w], T.rs[:, 0:w], ["rs"], ["rb%d" % s for s in ((1, 2), (3, 4), (5,))[k]], "av", n=w)
     cp(T.clu[:, 0:10], T.cli[:, 0:10], ["cl16"], ["c16"])
     cp(T.clu[:, 32:52], T.cli[:, 32:52], ["cl32"], ["c32"])
     cp(T.lt0[0:32, 0:10], T.cid[0:32, 0:10], CID, ["lt0_0"])
     ts(T.mlu[96:128, 1:20:2], T.cid[96:128, 0:10], 0.25, None, OP.mult, None, CID, ["ml_o3"])
-    fill(T.ones[:], 1.0, ["ones"])
+    fill(T.ones[:], 1.0, ["ones"], n=256)
+
+    def one_in(b):
+        op("g", lambda e: e.affine_select(T.et[:, 512 * b:512 * b + 512], T.ones[:], [[1, 512]], OP.is_equal, 0.0, -b, -4), ["ones"], ["et%d" % b], 1.2)
+
     for b in range(4):
-        op("g", lambda e: e.affine_select(T.et[:, 512 * b:512 * b + 512], T.ones[:], [[1, 512]], OP.is_equal, 0.0, -b, -4), ["ones"], ["et%d" % b])
+        one_in(b)
 
     def half_x(k, h):
-        x = T["x%d" % k]
         for n in ("xh", "xg"):
-            op("a", lambda e: e.activation(T[n][:, 640 * h:640 * h + 640], x[:, 640 * h:640 * h + 640], AF.Copy, scale=0.5), ["x%d%d" % (k, h)], ["%s%d" % (n, h)])
+            scaled(T[n][:, 640 * h:640 * h + 640], T["x%d" % k][:, 640 * h:640 * h + 640], 0.5, state_parts(k, h), ["%s%d" % (n, h)], "av", 640, 0.5)
 
-    window(3, "a")
+    def state_parts(k, h):
+        return ["x0%d" % h] if k == 0 else ["xn%d%d%d" % (k, h, t) for t in range(4)]
+
     half_x(0, 0)
     half_x(0, 1)
-    window(4, "a")
-    window(5, "a")
 
     def scores(k, h):
         mm(h, 160, T.utq[:], T.uts[:], T["qx%d" % k][:, 160 * h:160 * h + 160], T["sx%d" % k][:, 160 * h:160 * h + 160], ["utq", "uts", "qx%d%d" % (k, h)])
-        tr(T.st[:, 160 * h:160 * h + 160], bank(h, 160), ["b%d" % h], ["st%d" % h])
+        tr(T.st[:, 160 * h:160 * h + 160], bank(h, 160), ["b%d" % h], ["st%d" % h], 160)
 
     ST = ["st0", "st1"]
 
@@ -284,22 +357,36 @@ def rank_program(g, core, T, topo):
     def rstart(s):
         return T.rb[:, 160 * (s - 1):160 * s:16]
 
-    def flips(k, first):
-        qx, sx = T["qx%d" % k], T["sx%d" % k]
-        for s in range(6):
-            mm(2 + s, 320, T.ufq[:, 128 * s:128 * s + 128], T.ufs[:, 128 * s:128 * s + 128], qx[:], sx[:], ["ufq", "ufs", "qx%d0" % k, "qx%d1" % k])
-        for s in range(6):
-            if first:
-                for j, sg in ((0, T.sgn), (1, T.sgc)):
-                    o = T.nw[:, 640 * s + 320 * j:640 * s + 320 * j + 320]
-                    op("a", lambda e: e.activation(o, bank(2 + s, 320), AF.Sign, bias=EPS if j else -EPS, scale=sg[:, s:s + 1]), ["b%d" % (2 + s), "sgc"], ["nw%d%d" % (s, j)])
-            else:
-                op("a", lambda e: e.activation(T.sg2[:, 320 * s:320 * s + 320], bank(2 + s, 320), AF.Sign, bias=EPS, scale=T.sgc[:, s:s + 1]), ["b%d" % (2 + s), "sgc"], ["sg2%d" % s])
+    def sign(s, j):
+        o, i, sg = T.nw[:, 640 * s + 320 * j:640 * s + 320 * j + 320], bank(2 + s, 320), (T.sgn, T.sgc)[j][:, s:s + 1]
+        eps = EPS if j else -EPS
+        op("a", lambda e: e.activation(o, i, AF.Sign, bias=eps, scale=sg), ["b%d" % (2 + s), "sgc"], ["nw%d%d" % (s, j)], 0.33)
 
-    def both(s):
-        p = T.nw[:, 640 * s + 320:640 * s + 640]
-        tt(p, p, T.sg2[:, 320 * s:320 * s + 320], OP.mult, ["nw%d1" % s, "sg2%d" % s], ["nw%d1" % s])
-        op("a", lambda e: e.activation(T.nw[:, 640 * s:640 * s + 320], p, AF.Copy, scale=-1.0), ["nw%d1" % s], ["nw%d0" % s])
+    def flips(k):
+        for s in range(6):
+            mm(2 + s, 320, T.ufq[:, 128 * s:128 * s + 128], T.ufs[:, 128 * s:128 * s + 128], T["qx%d" % k][:], T["sx%d" % k][:], ["ufq", "ufs", "qx%d0" % k, "qx%d1" % k])
+        for s in range(6):
+            sign(s, 0)
+            sign(s, 1)
+
+    def turn_windows():
+        for s in range(6):
+            ts(T.fb[:, 10 * s:10 * s + 10], row(10 + s), T.sgc[:, s:s + 1], 0.0, OP.mult, OP.is_lt, ST + ["sgc"], ["fb%d" % s])
+        pairs = []
+        for a in range(4):
+            for b in (0, 1):
+                for c in (0, 1):
+                    p, q = 32 * a + 16 * b, 32 * a + 16 * c
+                    pairs.append((T.fx[q:q + 16, 60 * b:60 * b + 60], T.fb[p:p + 16, :]))
+        dma("s", pairs, ["fb%d" % s for s in range(6)], ["fx"], "dfx")
+        for k, (base, f) in enumerate(((T.cw, OP.add), (T.cx, OP.subtract))):
+            for b in (0, 1):
+                tt(T.fl[:, 120 * k + b:120 * k + 120:2], base[:, b:120:2], T.fx[:, 60 * b:60 * b + 60], f, ["fx", "cw", "cx"], ["fl%d%d" % (k, b)], n=60)
+            cp(T.flu[:, 128 * k:128 * k + 120], T.fl[:, 120 * k:120 * k + 120], ["fl%d0" % k, "fl%d1" % k], ["flu%d" % k], n=120)
+        for s in range(6):
+            for k in (0, 1):
+                cp(T.tx[:, 640 * s + k:640 * s + 640:2], T.tw[:, 640 * s:640 * s + 640].indirect(T.flu[:, 128 * k + 20 * s:128 * k + 20 * s + 20]),
+                   ["flu%d" % k, "tw%d" % s], ["tx%d%d" % (s, k)], "av", n=320, x=True)
 
     def direct(n, rd):
         dv = (T.dva, T.dvb)[n][:, 0:10]
@@ -310,7 +397,7 @@ def rank_program(g, core, T, topo):
             tt(tmp(o), tmp(o), T.cid[:, 0:10], OP.add, ["t%d" % o] + CID, ["t%d" % o])
             lin(T.nu[:, 96 + 16 * n:106 + 16 * n], tmp(o), 0.5, -640, ["t%d" % o], ["nu%d" % (6 + n)])
             tt(T.ye[:, 160 * n:160 * n + 160], T.tw[:, 640 * (6 + n):640 * (7 + n)].indirect(T.nu[:, 96 + 16 * n:106 + 16 * n]), mask1, OP.mult,
-               ["tw%d" % (6 + n), "nu%d" % (6 + n), "mask"], ["ye%d" % n])
+               ["tw%d" % (6 + n), "nu%d" % (6 + n), "mask"], ["ye%d" % n], n=160, x=True)
             scan(T.yes[:, 160 * n:160 * n + 160], rst1, T.ye[:, 160 * n:160 * n + 160], OP.min, OP.add, ["rs", "ye%d" % n], ["yes%d" % n])
             cp(dv, T.yes[:, 160 * n + 15:160 * n + 160:16], ["yes%d" % n], [name])
         else:
@@ -344,18 +431,14 @@ def rank_program(g, core, T, topo):
         tt(tmp(10), tmp(10), T.dva[:, 0:10], OP.add, ["t10", "dva"], ["t10"])
         lin(lu(0), tmp(10), cm, cb, ["t10"], ["lu0a"])
         if fl:
-            tt(T.y2i[:], T.dva[:, 0:10].indirect(T.clu[:, 0:10]), mask1, OP.mult, ["dva", "c16", "mask"], ["y2i"])
-        if rd == 3:
-            both(0)
-            both(1)
+            tt(T.y2i[:], T.dva[:, 0:10].indirect(T.clu[:, 0:10]), mask1, OP.mult, ["dva", "c16", "mask"], ["y2i"], n=160, x=True)
+        tabs = T.tx if rd == 3 else T.tw
         for s in range(6):
             L = ["lu%d%s" % (s, c) for c in "abc"]
-            if rd == 3 and s + 2 < 6:
-                both(s + 2)
             prev = "y2i" if s == 0 else "y2%d" % (s - 1)
             if fl:
                 pv = T.y2i[:] if s == 0 else T.y2[:, 160 * (s - 1):160 * s]
-                tt(T.y1[:], T.nw[:, 640 * s:640 * s + 640].indirect(lu(s)), pv, OP.add, L + ["nw%d0" % s, "nw%d1" % s, prev, prev + "x"], ["y1"])
+                tt(T.y1[:], T.nw[:, 640 * s:640 * s + 640].indirect(lu(s)), pv, OP.add, L + ["nw%d0" % s, "nw%d1" % s, prev, prev + "x"], ["y1"], n=160, x=True)
             if s < 5:
                 bits(s + 1)
             if fl:
@@ -366,9 +449,10 @@ def rank_program(g, core, T, topo):
             else:
                 lst = lu(s)
             y2, y2s = T.y2[:, 160 * s:160 * s + 160], T.y2s[:, 160 * s:160 * s + 160]
-            tt(y2, T.tw[:, 640 * s:640 * s + 640].indirect(lst), mask1, OP.mult, L + ["tw%d" % s, "mask"], ["y2%d" % s, "y2%dx" % s])
+            tt(y2, tabs[:, 640 * s:640 * s + 640].indirect(lst), mask1, OP.mult, L + (["tx%d0" % s, "tx%d1" % s] if rd == 3 else ["tw%d" % s]) + ["mask"],
+               ["y2%d" % s, "y2%dx" % s], n=160, x=True)
             rs = T.rb[:, 160 * s:160 * s + 160] if s < 5 else rst1
-            scan(y2s, rs, y2, OP.min, OP.add, ["y2%d" % s, "rb%d" % (s + 1), "rs"], ["y2s%d" % s])
+            scan(y2s, rs, y2, OP.min, OP.add, ["y2%d" % s, "y2%dx" % s, "rb%d" % (s + 1), "rs"], ["y2s%d" % s])
 
             def last(lo, hi):
                 return T.y2s[lo:hi, 160 * s + 15:160 * s + 160:16]
@@ -382,7 +466,7 @@ def rank_program(g, core, T, topo):
                     lin(T.lu[lo:hi, n:n + 10], last(lo, hi), cm, cb, ["y2s%d" % s], ["lu%d%s" % (s + 1, "ab"[k])])
             if s in (1, 3) and fl:
                 lo = 32 if s == 1 else 64
-                cp(T.y2[lo:lo + 32, 160 * s:160 * s + 160], T.y2b[lo:lo + 32, :], ["y2b", "y2%d" % s], ["y2%dx" % s])
+                cp(T.y2[lo:lo + 32, 160 * s:160 * s + 160], T.y2b[lo:lo + 32, :], ["y2b", "y2%d" % s], ["y2%dx" % s], n=160)
             lo = 32 * (1 + s // 2)
             lt = (T.lt0, T.lt1)[s % 2]
             if s < 5:
@@ -394,7 +478,7 @@ def rank_program(g, core, T, topo):
                 cp(T.lt1[0:32, 0:10], T.dvb[0:32, 0:10], ["dvb"], ["lt1_0"])
                 lin(T.mlu[96:128, 0:20:2], T.dvb[96:128, 0:10], 0.25, -320, ["dvb"], ["ml_e3"])
                 if fl:
-                    tt(T.y2b[:], T.dvb[:, 0:10].indirect(T.clu[:, 0:10]), mask1, OP.mult, ["dvb", "c16", "mask"], ["y2b"])
+                    tt(T.y2b[:], T.dvb[:, 0:10].indirect(T.clu[:, 0:10]), mask1, OP.mult, ["dvb", "c16", "mask"], ["y2b"], n=160, x=True)
             if s in (0, 2):
                 k = s + 2
                 lo = 16 * k
@@ -408,15 +492,15 @@ def rank_program(g, core, T, topo):
                 tt(T.tmp[0:96, 192:202], last(0, 96), rst(0, 96), OP.subtract, ["y2s4", "rb5"], ["t12"])
                 ts(T.mlu[0:96, 1:20:2], T.tmp[0:96, 192:202], 0.25, None, OP.mult, None, ["t12"], ["ml_o"])
                 op("a", lambda e: e.activation(T.bc0[:], T.lt0[:, 0:10].indirect(T.clu[:, 32:52]), AF.Copy, bias=-480.0, scale=0.25),
-                   ["c32"] + ["lt0_%d" % a for a in range(4)], ["bc0"])
+                   ["c32"] + ["lt0_%d" % a for a in range(4)], ["bc0"], us(320, 1, True))
             if s == 5:
                 op("v", lambda e: e.tensor_scalar(T.bc1[:], T.lt1[:, 0:10].indirect(T.clu[:, 32:52]), 0.25, -480.0, OP.mult, OP.add),
-                   ["c32"] + ["lt1_%d" % a for a in range(4)], ["bc1"])
+                   ["c32"] + ["lt1_%d" % a for a in range(4)], ["bc1"], us(320, 1, True))
                 lin(T.mlu[0:96, 0:20:2], last(0, 96), 0.25, -320, ["y2s5"], ["ml_e"])
-        tr(T.lw[:, 0:320], T.bc0[:], ["bc0"], ["lw0"])
-        tr(T.lw[:, 320:640], T.bc1[:], ["bc1"], ["lw1"])
-        cp(T.km[:], T.lw[:].indirect(T.mlu[:, 0:20]), ["lw0", "lw1", "ml_e", "ml_o", "ml_e3", "ml_o3"], ["km"])
-        tr(T.kt[:], T.km[:], ["km"], ["kt"])
+        tr(T.lw[:, 0:320], T.bc0[:], ["bc0"], ["lw0"], 320, 0.5)
+        tr(T.lw[:, 320:640], T.bc1[:], ["bc1"], ["lw1"], 320, 0.5)
+        cp(T.km[:], T.lw[:].indirect(T.mlu[:, 0:20]), ["lw0", "lw1", "ml_e", "ml_o", "ml_e3", "ml_o3"], ["km"], n=320, x=True)
+        tr(T.kt[:], T.km[:], ["km"], ["kt"], 320, 0.5)
         for t in range(4):
             lin(T.of[:, 32 * t:32 * t + 20], T.kt[:, 0:320:16], 4, 640 + t, ["kt"], ["of%d" % t])
         lin(T["kl%d" % rd][:], T.kt[:, 0:320:16], 1, 160, ["kt"], ["kl%d" % rd])
@@ -425,25 +509,25 @@ def rank_program(g, core, T, topo):
 
     def send(rd, what, h):
         dst = T.cores[rank ^ STEP[rd - 1]]
-        if what == "k":
-            need("g", deps_of(["kl%d" % rd], []))
-        else:
-            need("g", deps_of(["qh%d%d" % (rd, h)], []))
+        def put(fn, cost, late, land, sem, inc, own):
+            sent[0] += own
+            node({"g": fn}, {"g": cost}, late, ["kl%d" % rd if what == "k" else "qh%d%d" % (rd, h)], [land], sem, inc)
+
         q, s, lq, ls = T["qh%d" % rd], T["sh%d" % rd], T["lq%d" % rd], T["ls%d" % rd]
         if topo.may_write(core, dst):
             rid, pid = topo.addr(dst, core)
             m, n = topo.mask(core, dst), len(topo.engines(core, dst))
             if what == "k":
-                g.remote_dma(T["kr%d" % rd][:], T["kl%d" % rd][:], T.sem["kr%d" % rd], T.sem.lsem, pid, rid, m)
-                sent[0] += n
-                wrote["kr%d" % rd] = ("kr%d" % rd, n)
+                put(lambda e: e.remote_dma(T["kr%d" % rd][:], T["kl%d" % rd][:], T.sem["kr%d" % rd], T.sem.lsem, pid, rid, m), 1.0, 2.5, "kr%d" % rd, "kr%d" % rd, n, n)
                 return
             a = 160 * h
             sem = T.sem["ar%d%d" % (rd, h)]
-            g.remote_dma(lq[:, a:a + 160].bitcast(dt.uint8), q[:, a:a + 160].bitcast(dt.uint8), sem, T.sem.lsem, pid, rid, m)
-            g.remote_dma(ls[:, a:a + 160], s[:, a:a + 160], sem, T.sem.lsem, pid, rid, m)
-            sent[0] += 2 * n
-            wrote["lq%d%d" % (rd, h)] = ("ar%d%d" % (rd, h), 2 * n)
+
+            def go(e):
+                e.remote_dma(lq[:, a:a + 160].bitcast(dt.uint8), q[:, a:a + 160].bitcast(dt.uint8), sem, T.sem.lsem, pid, rid, m)
+                e.remote_dma(ls[:, a:a + 160], s[:, a:a + 160], sem, T.sem.lsem, pid, rid, m)
+
+            put(go, 2.0, 4.0, "lq%d%d" % (rd, h), "ar%d%d" % (rd, h), 2 * n, 2 * n)
             return
         rel = relays_of(core, dst, topo)
         ways = [topo.addr(k, core) for k in rel]
@@ -452,28 +536,27 @@ def rank_program(g, core, T, topo):
         masks = [bits_of(eng[:n]), bits_of(eng[n:])]
         far = len(topo.engines(rel[0], dst))
         if what == "k":
-            g.remote_dma(T.rlk[:], T["kl%d" % rd][:], T.sem.rk, T.sem.lsem, ways[0][1], ways[0][0], masks[0])
-            sent[0] += n
-            wrote["kr%d" % rd] = ("kr%d" % rd, far)
+            put(lambda e: e.remote_dma(T.rlk[:], T["kl%d" % rd][:], T.sem.rk, T.sem.lsem, ways[0][1], ways[0][0], masks[0]), 1.0, 5.0, "kr%d" % rd, "kr%d" % rd, far, n)
             return
 
-        def both_ways(view, land):
+        def both_ways(e, view, land):
             tr_ = []
             for k in (0, 1):
                 a = 160 * h + 80 * k
                 tr_.append(RemoteDMATransfer(dst_ids=[DstId(rid=ways[k][0], pnc=ways[k][1])], dma_engine_mask=masks[k], remote_sem=T.sem["ry%d" % h],
                                              src=view(a), dst=land(a)))
-            g.remote_dma_fused(tr_, local_sem=T.sem.lsem)
-            sent[0] += 2 * n
+            e.remote_dma_fused(tr_, local_sem=T.sem.lsem)
 
-        both_ways(lambda a: q[:, a:a + 80].bitcast(dt.uint8), lambda a: T.rlq[:, a:a + 80].bitcast(dt.uint8))
-        both_ways(lambda a: s[:, a:a + 80], lambda a: T.rls[:, a:a + 80])
-        wrote["lq%d%d" % (rd, h)] = ("ar%d%d" % (rd, h), 4 * far)
+        def go2(e):
+            both_ways(e, lambda a: q[:, a:a + 80].bitcast(dt.uint8), lambda a: T.rlq[:, a:a + 80].bitcast(dt.uint8))
+            both_ways(e, lambda a: s[:, a:a + 80], lambda a: T.rls[:, a:a + 80])
+
+        put(go2, 2.0, 6.0, "lq%d%d" % (rd, h), "ar%d%d" % (rd, h), 4 * far, 4 * n)
 
     def meet(h):
         for t in range(4):
             tt(T.vt[:, 640 * h + t:640 * h + 640:4], T.xh[:].indirect(T.of[:, 32 * t + 10 * h:32 * t + 10 * h + 10]), T.xg[:, 640 * h + t:640 * h + 640:4], OP.add,
-               ["xh0", "xh1", "xg%d" % h, "of%d" % t], ["vt%d%d" % (h, t)])
+               ["xh0", "xh1", "xg%d" % h, "of%d" % t] + ["@v"] * h, ["vt%d%d" % (h, t)], n=160, x=True)
 
     def layer(h):
         c = slice(160 * h, 160 * h + 160)
@@ -481,14 +564,10 @@ def rank_program(g, core, T, topo):
             mm(4 * h + b, 160, T.wq[:, 128 * b:128 * b + 128], T.wsp[:, 128 * b:128 * b + 128], T.qv[:, c], T.qvs[:, c], ["wq", "qv%d" % h])
 
     def layer_out(h, b, q):
-        o, i = T.ht[:, 640 * h + b:640 * h + 640:4], bank(4 * h + b, 160)
-        if q == "a":
-            op("a", lambda e: e.activation(o, i, AF.Copy, scale=0.03125), ["b%d" % (4 * h + b)], ["ht%d%d" % (h, b)])
-        else:
-            ts(o, i, 0.03125, None, OP.mult, None, ["b%d" % (4 * h + b)], ["ht%d%d" % (h, b)])
+        scaled(T.ht[:, 640 * h + b:640 * h + 640:4], bank(4 * h + b, 160), 0.03125, ["b%d" % (4 * h + b)], ["ht%d%d" % (h, b)], q, 160)
 
     def quant_v(h):
-        quant(T.qv[:, 160 * h:160 * h + 160], T.qvs[:, 160 * h:160 * h + 160], T.vt[:, 640 * h:640 * h + 640], ["vt%d%d" % (h, t) for t in range(4)], ["qv%d" % h])
+        quant(T.qv[:, 160 * h:160 * h + 160], T.qvs[:, 160 * h:160 * h + 160], T.vt[:, 640 * h:640 * h + 640], ["vt%d%d" % (h, t) for t in range(4)], ["qv%d" % h] + ["@v"] * (1 - h))
 
     def quant_h(rd, h):
         quant(T["qh%d" % rd][:, 160 * h:160 * h + 160], T["sh%d" % rd][:, 160 * h:160 * h + 160], T.ht[:, 640 * h:640 * h + 640],
@@ -496,7 +575,7 @@ def rank_program(g, core, T, topo):
 
     def natural(k, rd):
         mm(0, 320, T.uq[:], T.us[:], T["qx%d" % k][:], T["sx%d" % k][:], ["uq", "qx%d0" % k, "qx%d1" % k])
-        cp(T.sn[:], bank(0, 320), ["b0"], ["sn"], "a")
+        cp(T.sn[:], bank(0, 320), ["b0"], ["sn"], "av", n=320)
         dma("s", [(T.fn[:], T.sn[1:128:16, :])], ["sn"], ["fn"], "fn%d" % rd)
 
     def turn_tables():
@@ -504,7 +583,7 @@ def rank_program(g, core, T, topo):
             n = "lr%d" % k
             a, b = T.lt2[:, 32 * k:32 * k + 20], n + "t"
             e0, e1 = tab[:, 0:40:2], tab[:, 1:40:2]
-            z = T.qf[:, 32 * k:32 * k + 20]
+            z = T.lz[:, 32 * k:32 * k + 20]
             ts(a, T.fn[:], 0.0, None, f, None, ["fn"], [b])
             tt(z, e1, e0, OP.subtract, [n], [n + "z"])
             tt(z, z, a, OP.mult, [n + "z", b], [n + "z"])
@@ -513,7 +592,6 @@ def rank_program(g, core, T, topo):
 
     for h in (0, 1):
         scores(0, h)
-    window(7, "v")
     for rd in (1, 2, 3):
         walk(rd)
         send(rd, "k", 0)
@@ -521,18 +599,18 @@ def rank_program(g, core, T, topo):
         quant_v(0)
         layer(0)
         for b in range(4):
-            layer_out(0, b, "a")
+            layer_out(0, b, "av")
         meet(1)
         quant_v(1)
         layer(1)
         quant_h(rd, 0)
         send(rd, "h", 0)
         for b in range(4):
-            layer_out(1, b, "av"[b % 2])
+            layer_out(1, b, "av")
         quant_h(rd, 1)
         send(rd, "h", 1)
         if rd == 1:
-            quant(T.eq[:], T.es[:], T.et[:], ["et%d" % b for b in range(4)], ["eq"])
+            quant(T.eq[:], T.es[:], T.et[:], ["et%d" % b for b in range(4)], ["eq"], n=2048)
             for s in range(6):
                 fill(T.ui[:, 8 * s + 2 * (s // 2 + 1):8 * s + 8], 16 * (s + 1) + 1, ["ui"])
             cp(T.uoff[:, 8:56], T.ui[:, 0:48], ["ui"], ["uoff2"])
@@ -543,36 +621,33 @@ def rank_program(g, core, T, topo):
             fill(T.sgc[32:64, 7:8], -1.0, ["sgc"])
             fill(T.sgc[64:128, 7:8], -1.0, ["sgc"])
             ts(T.sgn[:], T.sgc[:], -1.0, None, OP.mult, None, ["sgc"], ["sgc"])
-            cp(T.ufq[:].bitcast(dt.uint32), T.uq[:, 0:128].bitcast(dt.uint32).indirect(T.uoff[:, 8:56]), ["uq", "uoff2"], ["ufq"])
-            cp(T.ufs[:], T.us[:, 0:128].indirect(T.uoff[:, 8:56]), ["uq", "uoff2"], ["ufs"], "a")
+            cp(T.ufq[:].bitcast(dt.uint32), T.uq[:, 0:128].bitcast(dt.uint32).indirect(T.uoff[:, 8:56]), ["uq", "uoff2"], ["ufq"], n=768, x=True)
+            cp(T.ufs[:], T.us[:, 0:128].indirect(T.uoff[:, 8:56]), ["uq", "uoff2"], ["ufs"], "av", n=768, x=True)
             for n in (0, 1):
                 for c in (0, 1):
                     k = 2 * n + c
                     if n == 0:
                         lin(T.lu[:, 96 + 16 * c:106 + 16 * c], T.cid[:, 0:10], 0.5, -640 + c, CID, ["lc%d" % c])
                     tt(T.ye[:, 160 * k:160 * k + 160], T.tw[:, 640 * (6 + n):640 * (7 + n)].indirect(T.lu[:, 96 + 16 * c:106 + 16 * c]), mask1, OP.mult,
-                       ["tw%d" % (6 + n), "lc%d" % c, "mask"], ["ye%d" % k])
+                       ["tw%d" % (6 + n), "lc%d" % c, "mask"], ["ye%d" % k], n=160, x=True)
                     scan(T.yes[:, 160 * k:160 * k + 160], rst1, T.ye[:, 160 * k:160 * k + 160], OP.min, OP.add, ["rs", "ye%d" % k], ["yes%d" % k])
                 e, d = (T.ea, T.eb)[n][:, 0:10], (T.da, T.db)[n][:, 0:10]
                 first, second = T.yes[:, 320 * n + 15:320 * n + 160:16], T.yes[:, 320 * n + 175:320 * n + 320:16]
                 cp(e, first, ["yes%d" % (2 * n)], ["e%d" % n])
                 tt(d, second, first, OP.subtract, ["yes%d" % (2 * n), "yes%d" % (2 * n + 1)], ["d%d" % n])
-            cp(T.lnu[:], T.lni[:], ["lni"], ["lnu"])
-        else:
-            natural(rd - 1, rd - 1)
-            if rd == 2:
-                turn_direct(0)
-                turn_direct(1)
-            turn_tables()
+            cp(T.lnu[:], T.lni[:], ["lni"], ["lnu"], n=80)
+        elif rd == 2:
+            turn_direct(0)
+            turn_direct(1)
         kl, kr = T["kl%d" % rd], T["kr%d" % rd]
-        cp(T.kw[:], T.w4[:].indirect(kr[:]), ["w4", "kr%d" % rd], ["kw"], "a")
-        tt(T.ky[:], T.kw[:].indirect(kl[:]), T.mask[:], OP.mult, ["kw", "kl%d" % rd, "mask"], ["ky"])
-        scan(T.kys[:], T.rs[:], T.ky[:], OP.min, OP.add, ["ky", "rs"], ["kys"])
+        cp(T.kw[:], T.w4[:].indirect(kr[:]), ["w4", "kr%d" % rd], ["kw"], "av", n=320, x=True)
+        tt(T.ky[:], T.kw[:].indirect(kl[:]), T.mask[:], OP.mult, ["kw", "kl%d" % rd, "mask"], ["ky"], n=320, x=True)
+        scan(T.kys[:], T.rs[:], T.ky[:], OP.min, OP.add, ["ky", "rs"], ["kys"], n=320)
         for t in range(4):
             lin(T.mo[:, 32 * t:32 * t + 20], T.kys[:, 15:320:16], 1, -1280 + t, ["kys"], ["mo%d" % t])
         if rd == 1:
             for k, tgt in ((0, T.lrow), (1, T.rrow)):
-                cp(tgt[:], T.w4[:].indirect(T.lnu[:, 40 * k:40 * k + 40]), ["w4", "lnu"], ["row%d" % k], "a")
+                cp(tgt[:], T.w4[:].indirect(T.lnu[:, 40 * k:40 * k + 40]), ["w4", "lnu"], ["row%d" % k], "av", n=640, x=True)
                 dma("s", [((T.ltb, T.rtb)[k][:], tgt[0:128:16, :])], ["row%d" % k], ["lr%d" % k], "dt%d" % k)
         if rd == 3:
             quant(T.vq[:], T.vs[:], T.vb[:], ["vb"], ["vq"])
@@ -582,13 +657,13 @@ def rank_program(g, core, T, topo):
                 mm(4 * h + b, 160, T.eq[:, 128 * b:128 * b + 128], T.es[:, 128 * b:128 * b + 128], lq[:, 160 * h:160 * h + 160], ls[:, 160 * h:160 * h + 160],
                    ["eq", "lq%d%d" % (rd, h)])
             for b in range(4):
-                cp(T.dd[:, 640 * h + b:640 * h + 640:4], bank(4 * h + b, 160), ["b%d" % (4 * h + b)], ["dd%d%d" % (h, b)], "av"[b % 2])
+                cp(T.dd[:, 640 * h + b:640 * h + 640:4], bank(4 * h + b, 160), ["b%d" % (4 * h + b)], ["dd%d%d" % (h, b)], "av", n=160)
         xn, qn, sn = T["x%d" % rd], T["qx%d" % rd], T["sx%d" % rd]
         for h in (0, 1):
             for t in range(4):
                 tt(xn[:, 640 * h + t:640 * h + 640:4], T.dd[:].indirect(T.mo[:, 32 * t + 10 * h:32 * t + 10 * h + 10]), T.vt[:, 640 * h + t:640 * h + 640:4], OP.add,
-                   ["mo%d" % t, "vt%d%d" % (h, t)] + ["dd%d%d" % (i, b) for i in (0, 1) for b in range(4)], ["x%d%d" % (rd, h), "xn%d%d%d" % (rd, h, t)])
-            quant(qn[:, 160 * h:160 * h + 160], sn[:, 160 * h:160 * h + 160], xn[:, 640 * h:640 * h + 640], ["x%d%d" % (rd, h)] + ["xn%d%d%d" % (rd, h, t) for t in range(4)], ["qx%d%d" % (rd, h)])
+                   ["mo%d" % t, "vt%d%d" % (h, t)] + ["@x"] * h + ["dd%d%d" % (i, b) for i in (0, 1) for b in range(4)], ["xn%d%d%d" % (rd, h, t)], n=160, x=True)
+            quant(qn[:, 160 * h:160 * h + 160], sn[:, 160 * h:160 * h + 160], xn[:, 640 * h:640 * h + 640], state_parts(rd, h), ["qx%d%d" % (rd, h)] + ["@x"] * (1 - h))
             if rd == 3:
                 c = slice(160 * h, 160 * h + 160)
                 dma("s", [(T.oc[:, 640 * h:640 * h + 640], qn[:, c].bitcast(dt.uint8))] + [(T.osc[4 * k:4 * k + 4, c], sn[32 * k:32 * k + 4, c]) for k in range(4)],
@@ -596,19 +671,21 @@ def rank_program(g, core, T, topo):
             else:
                 scores(rd, h)
         if rd < 3:
-            flips(rd, rd == 1)
+            flips(rd)
             half_x(rd, 0)
             half_x(rd, 1)
+            natural(rd, rd)
+            turn_tables()
+            if rd == 1:
+                turn_windows()
     natural(3, 3)
     mm(1, 320, T.vq[:], T.vs[:], T.qx3[:], T.sx3[:], ["vq", "qx30", "qx31"])
-    cp(T.yb[:], bank(1, 320), ["b1"], ["yb"])
+    cp(T.yb[:], bank(1, 320), ["b1"], ["yb"], "av", n=320)
     dma("s", [(T.y[:], T.yb[:])], ["yb"], [], "oy")
     turn_tables()
     for k, tab in enumerate((T.ltb, T.rtb)):
         lin(T.lout[:, 40 * k:40 * k + 40], tab[:], 0.25, -320, ["lr%d" % k], ["lo%d" % k])
         dma("s", [(T.lr[:, 640 * k:640 * k + 640], T.lout[:, 40 * k:40 * k + 40])], ["lo%d" % k], [], "ol")
+    issue()
     need("g", dict(total))
     g.wait_ge(T.sem.lsem, sent[0])
-    for rd in (1, 2, 3):
-        for k in ("kr%d" % rd, "lq%d0" % rd, "lq%d1" % rd):
-            need("g", {wrote[k][0]: wrote[k][1]})

@@ -26,15 +26,30 @@ for _n, _w, _d in [
     ("cid", 16, F), ("dva", 16, F), ("dvb", 16, F), ("ea", 16, F), ("da", 16, F), ("eb", 16, F), ("db", 16, F), ("tmp", 256, F),
     ("y1", 160, F), ("y1s", 160, F), ("y2i", 160, F), ("y2b", 160, F), ("y2", 960, F), ("y2s", 960, F), ("ye", 640, F), ("yes", 640, F),
     ("lu", 128, U), ("nu", 128, U), ("lt0", 16, F), ("lt1", 16, F), ("bc0", 320, B), ("bc1", 320, B), ("lw", 640, B), ("km", 320, B), ("kt", 320, B),
-    ("mlu", 32, U), ("of", 128, U), ("kl1", 20, U), ("kl2", 20, U), ("kl3", 20, U), ("kr1", 20, U), ("kr2", 20, U), ("kr3", 20, U), ("rlk", 20, U),
+    ("mlu", 32, U), ("ld", 64, F), ("kl1", 20, U), ("kl2", 20, U), ("kl3", 20, U), ("kr1", 20, U), ("kr2", 20, U), ("kr3", 20, U), ("rlk", 20, U),
     ("kw", 320, F), ("ky", 320, F), ("kys", 320, F), ("mo", 128, U),
     ("sn", 320, F), ("fn", 20, F), ("ltb", 40, F), ("rtb", 40, F), ("lrow", 640, F), ("rrow", 640, F), ("lni", 80, I), ("lnu", 80, U), ("lout", 80, F), ("lt2", 64, F),
     ("yb", 320, F), ("sgc", 8, F), ("sgn", 8, F), ("cli", 64, I), ("clu", 64, U), ("ui", 64, I), ("uf", 64, F), ("uoff", 64, U), ("qi", 16, I), ("qf", 128, F),
 ]:
     SCRATCH[_n] = ("sbuf", [128, _w], _d)
 
-SEMAPHORES = (["sv", "sa", "st", "sg", "dx0", "dx1", "du", "dv", "dw", "dl", "dt0", "dt1", "fn1", "fn2", "fn3", "oy", "ol", "oq0", "oq1", "dfx", "lsem", "ry0", "ry1", "rk"]
+SEMAPHORES = (["sv", "sa", "st", "sg", "dx0", "dx1", "du", "dv", "dw", "dl", "dt0", "dt1", "fn1", "fn2", "fn3", "oy", "ol", "oq0", "oq1", "dfx", "lsem", "ry0", "ry1", "rz0", "rz1", "rk"]
               + ["dn%d" % s for s in range(8)] + ["ar%d%d" % (r, h) for r in (1, 2, 3) for h in (0, 1)] + ["kr%d" % r for r in (1, 2, 3)])
+
+
+AT, WID = (0, 160), (160, 160)
+
+
+def cols(h):
+    return slice(AT[h], AT[h] + WID[h])
+
+
+def quad(h, t=0, step=1):
+    return slice(4 * AT[h] + t, 4 * (AT[h] + WID[h]), step)
+
+
+def part(h):
+    return slice(AT[h] // 16, (AT[h] + WID[h]) // 16)
 
 
 def bits_of(engines):
@@ -67,10 +82,12 @@ def relay_program(g, core, T, topo):
             g.remote_dma(T.kr2[:], T.rlk[:], T.sem.kr2, T.sem.lsem, pid, rid, m)
             sent += n
         for h in (0, 1):
-            a = 160 * h + 80 * k
-            g.wait_ge(T.sem["ry%d" % h], 2 * half)
-            g.remote_dma(T.lq2[:, a:a + 80].bitcast(dt.uint8), T.rlq[:, a:a + 80].bitcast(dt.uint8), T.sem["ar2%d" % h], T.sem.lsem, pid, rid, m)
-            g.remote_dma(T.ls2[:, a:a + 80], T.rls[:, a:a + 80], T.sem["ar2%d" % h], T.sem.lsem, pid, rid, m)
+            w = WID[h] // 2
+            a = AT[h] + w * k
+            g.wait_ge(T.sem["ry%d" % h], half)
+            g.remote_dma(T.lq2[:, a:a + w].bitcast(dt.uint8), T.rlq[:, a:a + w].bitcast(dt.uint8), T.sem["ar2%d" % h], T.sem.lsem, pid, rid, m)
+            g.wait_ge(T.sem["rz%d" % h], half)
+            g.remote_dma(T.ls2[:, a:a + w], T.rls[:, a:a + w], T.sem["ar2%d" % h], T.sem.lsem, pid, rid, m)
             sent += 2 * n
         g.wait_ge(T.sem.lsem, sent)
 
@@ -229,7 +246,7 @@ def rank_program(g, core, T, topo):
     mask1, rst1 = T.mask[:, 0:160], T.rs[:, 0:160]
 
     for h in (0, 1):
-        dma("s", [(T.x0[:, 640 * h:640 * h + 640], T.x[:, 640 * h:640 * h + 640])], [], ["x0%d" % h], "dx%d" % h)
+        dma("s", [(T.x0[:, quad(h)], T.x[:, quad(h)])], [], ["x0%d" % h], "dx%d" % h)
     dma("a", [(T.ub[:], T.u[:])], [], ["ub"], "du")
     for k, s in enumerate((6, 0, 7, 1, 2, 3, 4, 5)):
         pairs = []
@@ -316,14 +333,14 @@ def rank_program(g, core, T, topo):
     ts(T.cw[:], T.cw[:], T.qf[:, 96:97], None, OP.add, None, ["cw", "q2"], ["cw"], n=120)
     lin(T.cx[:], T.cw[:], 1, 1, ["cw"], ["cx"], n=120)
     for h in (0, 1):
-        quant(T.qx0[:, 160 * h:160 * h + 160], T.sx0[:, 160 * h:160 * h + 160], T.x0[:, 640 * h:640 * h + 640], ["x0%d" % h], ["qx0%d" % h])
+        quant(T.qx0[:, cols(h)], T.sx0[:, cols(h)], T.x0[:, quad(h)], ["x0%d" % h], ["qx0%d" % h], 4 * WID[h])
     for k in range(3):
         w = 320 if k < 2 else 160
         cp(T.rb[:, 320 * k:320 * k + w], T.rs[:, 0:w], ["rs"], ["rb%d" % s for s in ((1, 2), (3, 4), (5,))[k]], "av", n=w)
     cp(T.clu[:, 0:10], T.cli[:, 0:10], ["cl16"], ["c16"])
     cp(T.clu[:, 32:52], T.cli[:, 32:52], ["cl32"], ["c32"])
     cp(T.lt0[0:32, 0:10], T.cid[0:32, 0:10], CID, ["lt0_0"])
-    ts(T.mlu[96:128, 1:20:2], T.cid[96:128, 0:10], 0.25, None, OP.mult, None, CID, ["ml_o3"])
+    cp(T.lt1[96:128, 0:10], T.cid[96:128, 0:10], CID, ["lt1_3"])
     fill(T.ones[:], 1.0, ["ones"], n=256)
 
     def one_in(b):
@@ -333,8 +350,11 @@ def rank_program(g, core, T, topo):
         one_in(b)
 
     def half_x(k, h):
-        for n in ("xh", "xg"):
-            scaled(T[n][:, 640 * h:640 * h + 640], T["x%d" % k][:, 640 * h:640 * h + 640], 0.5, state_parts(k, h), ["%s%d" % (n, h)], "av", 640, 0.5)
+        x = T["x%d" % k]
+        for t in range(4):
+            scaled(T.xh[:, 320 * t + AT[h]:320 * t + AT[h] + WID[h]], x[:, quad(h, t, 4)], 0.5, state_parts(k, h)[t % len(state_parts(k, h)):][:1],
+                   ["xh%d%d" % (h, t)], "av", WID[h], 0.5)
+        scaled(T.xg[:, quad(h)], x[:, quad(h)], 0.5, state_parts(k, h), ["xg%d" % h], "av", 4 * WID[h], 0.5)
 
     def state_parts(k, h):
         return ["x0%d" % h] if k == 0 else ["xn%d%d%d" % (k, h, t) for t in range(4)]
@@ -343,8 +363,8 @@ def rank_program(g, core, T, topo):
     half_x(0, 1)
 
     def scores(k, h):
-        mm(h, 160, T.utq[:], T.uts[:], T["qx%d" % k][:, 160 * h:160 * h + 160], T["sx%d" % k][:, 160 * h:160 * h + 160], ["utq", "uts", "qx%d%d" % (k, h)])
-        tr(T.st[:, 160 * h:160 * h + 160], bank(h, 160), ["b%d" % h], ["st%d" % h], 160)
+        mm(h, WID[h], T.utq[:], T.uts[:], T["qx%d" % k][:, cols(h)], T["sx%d" % k][:, cols(h)], ["utq", "uts", "qx%d%d" % (k, h)])
+        tr(T.st[:, cols(h)], bank(h, WID[h]), ["b%d" % h], ["st%d" % h], WID[h])
 
     ST = ["st0", "st1"]
 
@@ -416,6 +436,13 @@ def rank_program(g, core, T, topo):
         tt(d, d, tmp(o + 3), OP.subtract, ["d%d" % n, "t%d" % (o + 3)], ["d%d" % n])
         tt(d, d, tmp(o + 3), OP.subtract, ["d%d" % n, "t%d" % (o + 3)], ["d%d" % n])
 
+    def spread(j):
+        o, win, lst = (T.bc0, T.bc1)[j][:], (T.lt0, T.lt1)[j][:, 0:10], T.clu[:, 32:52]
+        node({"v": lambda e: e.tensor_scalar(o, win.indirect(lst), 0.25, -480.0, OP.mult, OP.add),
+              "a": lambda e: e.activation(o, win.indirect(lst), AF.Copy, bias=-480.0, scale=0.25)},
+             {"v": us(320, 1, True), "a": us(320, 1, True)}, 0.0, ["c32"] + ["lt%d_%d" % (j, a) for a in range(4)], ["bc%d" % j], None, 1)
+        tr(T.lw[:, 320 * j:320 * j + 320], o, ["bc%d" % j], ["lw%d" % j], 320, 0.5)
+
     def lu(s):
         return T.lu[:, 16 * s:16 * s + 10]
 
@@ -471,8 +498,6 @@ def rank_program(g, core, T, topo):
             lt = (T.lt0, T.lt1)[s % 2]
             if s < 5:
                 tt(lt[lo:lo + 32, 0:10], last(lo, lo + 32), rst(lo, lo + 32), OP.subtract, ["y2s%d" % s, "rb%d" % (s + 1)], ["lt%d_%d" % (s % 2, lo // 32)])
-            else:
-                cp(lt[lo:lo + 32, 0:10], last(lo, lo + 32), ["y2s5"], ["lt1_3"])
             if s == 0:
                 direct(1, rd)
                 cp(T.lt1[0:32, 0:10], T.dvb[0:32, 0:10], ["dvb"], ["lt1_0"])
@@ -491,18 +516,13 @@ def rank_program(g, core, T, topo):
             if s == 4:
                 tt(T.tmp[0:96, 192:202], last(0, 96), rst(0, 96), OP.subtract, ["y2s4", "rb5"], ["t12"])
                 ts(T.mlu[0:96, 1:20:2], T.tmp[0:96, 192:202], 0.25, None, OP.mult, None, ["t12"], ["ml_o"])
-                op("a", lambda e: e.activation(T.bc0[:], T.lt0[:, 0:10].indirect(T.clu[:, 32:52]), AF.Copy, bias=-480.0, scale=0.25),
-                   ["c32"] + ["lt0_%d" % a for a in range(4)], ["bc0"], us(320, 1, True))
+            if s in (3, 4):
+                spread(4 - s)
             if s == 5:
-                op("v", lambda e: e.tensor_scalar(T.bc1[:], T.lt1[:, 0:10].indirect(T.clu[:, 32:52]), 0.25, -480.0, OP.mult, OP.add),
-                   ["c32"] + ["lt1_%d" % a for a in range(4)], ["bc1"], us(320, 1, True))
+                ts(T.mlu[96:128, 1:20:2], last(96, 128), 0.25, None, OP.mult, None, ["y2s5"], ["ml_o3"])
                 lin(T.mlu[0:96, 0:20:2], last(0, 96), 0.25, -320, ["y2s5"], ["ml_e"])
-        tr(T.lw[:, 0:320], T.bc0[:], ["bc0"], ["lw0"], 320, 0.5)
-        tr(T.lw[:, 320:640], T.bc1[:], ["bc1"], ["lw1"], 320, 0.5)
         cp(T.km[:], T.lw[:].indirect(T.mlu[:, 0:20]), ["lw0", "lw1", "ml_e", "ml_o", "ml_e3", "ml_o3"], ["km"], n=320, x=True)
         tr(T.kt[:], T.km[:], ["km"], ["kt"], 320, 0.5)
-        for t in range(4):
-            lin(T.of[:, 32 * t:32 * t + 20], T.kt[:, 0:320:16], 4, 640 + t, ["kt"], ["of%d" % t])
         lin(T["kl%d" % rd][:], T.kt[:, 0:320:16], 1, 160, ["kt"], ["kl%d" % rd])
 
     sent = [0]
@@ -520,12 +540,12 @@ def rank_program(g, core, T, topo):
             if what == "k":
                 put(lambda e: e.remote_dma(T["kr%d" % rd][:], T["kl%d" % rd][:], T.sem["kr%d" % rd], T.sem.lsem, pid, rid, m), 1.0, 2.5, "kr%d" % rd, "kr%d" % rd, n, n)
                 return
-            a = 160 * h
+            c = cols(h)
             sem = T.sem["ar%d%d" % (rd, h)]
 
             def go(e):
-                e.remote_dma(lq[:, a:a + 160].bitcast(dt.uint8), q[:, a:a + 160].bitcast(dt.uint8), sem, T.sem.lsem, pid, rid, m)
-                e.remote_dma(ls[:, a:a + 160], s[:, a:a + 160], sem, T.sem.lsem, pid, rid, m)
+                e.remote_dma(lq[:, c].bitcast(dt.uint8), q[:, c].bitcast(dt.uint8), sem, T.sem.lsem, pid, rid, m)
+                e.remote_dma(ls[:, c], s[:, c], sem, T.sem.lsem, pid, rid, m)
 
             put(go, 2.0, 4.0, "lq%d%d" % (rd, h), "ar%d%d" % (rd, h), 2 * n, 2 * n)
             return
@@ -539,68 +559,69 @@ def rank_program(g, core, T, topo):
             put(lambda e: e.remote_dma(T.rlk[:], T["kl%d" % rd][:], T.sem.rk, T.sem.lsem, ways[0][1], ways[0][0], masks[0]), 1.0, 5.0, "kr%d" % rd, "kr%d" % rd, far, n)
             return
 
-        def both_ways(e, view, land):
+        w = WID[h] // 2
+
+        def both_ways(e, view, land, sem):
             tr_ = []
             for k in (0, 1):
-                a = 160 * h + 80 * k
-                tr_.append(RemoteDMATransfer(dst_ids=[DstId(rid=ways[k][0], pnc=ways[k][1])], dma_engine_mask=masks[k], remote_sem=T.sem["ry%d" % h],
+                a = AT[h] + w * k
+                tr_.append(RemoteDMATransfer(dst_ids=[DstId(rid=ways[k][0], pnc=ways[k][1])], dma_engine_mask=masks[k], remote_sem=sem,
                                              src=view(a), dst=land(a)))
             e.remote_dma_fused(tr_, local_sem=T.sem.lsem)
 
         def go2(e):
-            both_ways(e, lambda a: q[:, a:a + 80].bitcast(dt.uint8), lambda a: T.rlq[:, a:a + 80].bitcast(dt.uint8))
-            both_ways(e, lambda a: s[:, a:a + 80], lambda a: T.rls[:, a:a + 80])
+            both_ways(e, lambda a: q[:, a:a + w].bitcast(dt.uint8), lambda a: T.rlq[:, a:a + w].bitcast(dt.uint8), T.sem["ry%d" % h])
+            both_ways(e, lambda a: s[:, a:a + w], lambda a: T.rls[:, a:a + w], T.sem["rz%d" % h])
 
         put(go2, 2.0, 6.0, "lq%d%d" % (rd, h), "ar%d%d" % (rd, h), 4 * far, 4 * n)
 
-    def meet(h):
+    def meet(rd, h):
         for t in range(4):
-            tt(T.vt[:, 640 * h + t:640 * h + 640:4], T.xh[:].indirect(T.of[:, 32 * t + 10 * h:32 * t + 10 * h + 10]), T.xg[:, 640 * h + t:640 * h + 640:4], OP.add,
-               ["xh0", "xh1", "xg%d" % h, "of%d" % t] + ["@v"] * h, ["vt%d%d" % (h, t)], n=160, x=True)
+            tt(T.vt[:, quad(h, t, 4)], T.xh[:, 320 * t:320 * t + 320].indirect(T["kl%d" % rd][:, part(h)]), T.xg[:, quad(h, t, 4)], OP.add,
+               ["xh0%d" % t, "xh1%d" % t, "xg%d" % h, "kl%d" % rd] + ["@v"] * h, ["vt%d%d" % (h, t)], n=WID[h], x=True)
 
     def layer(h):
-        c = slice(160 * h, 160 * h + 160)
+        c = cols(h)
         for b in range(4):
-            mm(4 * h + b, 160, T.wq[:, 128 * b:128 * b + 128], T.wsp[:, 128 * b:128 * b + 128], T.qv[:, c], T.qvs[:, c], ["wq", "qv%d" % h])
+            mm(4 * h + b, WID[h], T.wq[:, 128 * b:128 * b + 128], T.wsp[:, 128 * b:128 * b + 128], T.qv[:, c], T.qvs[:, c], ["wq", "qv%d" % h])
 
     def layer_out(h, b, q):
-        scaled(T.ht[:, 640 * h + b:640 * h + 640:4], bank(4 * h + b, 160), 0.03125, ["b%d" % (4 * h + b)], ["ht%d%d" % (h, b)], q, 160)
+        scaled(T.ht[:, quad(h, b, 4)], bank(4 * h + b, WID[h]), 0.03125, ["b%d" % (4 * h + b)], ["ht%d%d" % (h, b)], q, WID[h])
 
     def quant_v(h):
-        quant(T.qv[:, 160 * h:160 * h + 160], T.qvs[:, 160 * h:160 * h + 160], T.vt[:, 640 * h:640 * h + 640], ["vt%d%d" % (h, t) for t in range(4)], ["qv%d" % h] + ["@v"] * (1 - h))
+        quant(T.qv[:, cols(h)], T.qvs[:, cols(h)], T.vt[:, quad(h)], ["vt%d%d" % (h, t) for t in range(4)], ["qv%d" % h] + ["@v"] * (1 - h), 4 * WID[h])
 
     def quant_h(rd, h):
-        quant(T["qh%d" % rd][:, 160 * h:160 * h + 160], T["sh%d" % rd][:, 160 * h:160 * h + 160], T.ht[:, 640 * h:640 * h + 640],
-              ["ht%d%d" % (h, b) for b in range(4)], ["qh%d%d" % (rd, h)])
+        quant(T["qh%d" % rd][:, cols(h)], T["sh%d" % rd][:, cols(h)], T.ht[:, quad(h)], ["ht%d%d" % (h, b) for b in range(4)], ["qh%d%d" % (rd, h)], 4 * WID[h])
 
     def natural(k, rd):
         mm(0, 320, T.uq[:], T.us[:], T["qx%d" % k][:], T["sx%d" % k][:], ["uq", "qx%d0" % k, "qx%d1" % k])
         cp(T.sn[:], bank(0, 320), ["b0"], ["sn"], "av", n=320)
         dma("s", [(T.fn[:], T.sn[1:128:16, :])], ["sn"], ["fn"], "fn%d" % rd)
 
-    def turn_tables():
+    def turn_tables(final=False):
         for k, (tab, f) in enumerate(((T.ltb, OP.is_lt), (T.rtb, OP.is_gt))):
             n = "lr%d" % k
-            a, b = T.lt2[:, 32 * k:32 * k + 20], n + "t"
+            a, d, z = T.lt2[:, 32 * k:32 * k + 20], T.ld[:, 32 * k:32 * k + 20], T.lz[:, 32 * k:32 * k + 20]
             e0, e1 = tab[:, 0:40:2], tab[:, 1:40:2]
-            z = T.lz[:, 32 * k:32 * k + 20]
-            ts(a, T.fn[:], 0.0, None, f, None, ["fn"], [b])
-            tt(z, e1, e0, OP.subtract, [n], [n + "z"])
-            tt(z, z, a, OP.mult, [n + "z", b], [n + "z"])
-            tt(e0, e0, z, OP.add, [n, n + "z"], [n])
-            tt(e1, e1, z, OP.subtract, [n, n + "z"], [n])
+            o = T.lout[:, 40 * k:40 * k + 40] if final else tab
+            tt(d, e1, e0, OP.subtract, [n + "a", n + "b"], [n + "d"])
+            ts(a, T.fn[:], 0.0, None, f, None, ["fn"], [n + "t"])
+            tt(z, d, a, OP.mult, [n + "d", n + "t"], [n + "z"])
+            tt(o[:, 0:40:2], e0, z, OP.add, [n + "a", n + "z"], [("lo%da" % k) if final else n + "a"])
+            tt(o[:, 1:40:2], e1, z, OP.subtract, [n + "b", n + "z"], [("lo%db" % k) if final else n + "b"])
 
     for h in (0, 1):
         scores(0, h)
     for rd in (1, 2, 3):
         walk(rd)
         send(rd, "k", 0)
-        meet(0)
+        meet(rd, 0)
         quant_v(0)
         layer(0)
         for b in range(4):
             layer_out(0, b, "av")
-        meet(1)
+        meet(rd, 1)
         quant_v(1)
         layer(1)
         quant_h(rd, 0)
@@ -643,30 +664,32 @@ def rank_program(g, core, T, topo):
         cp(T.kw[:], T.w4[:].indirect(kr[:]), ["w4", "kr%d" % rd], ["kw"], "av", n=320, x=True)
         tt(T.ky[:], T.kw[:].indirect(kl[:]), T.mask[:], OP.mult, ["kw", "kl%d" % rd, "mask"], ["ky"], n=320, x=True)
         scan(T.kys[:], T.rs[:], T.ky[:], OP.min, OP.add, ["ky", "rs"], ["kys"], n=320)
-        for t in range(4):
-            lin(T.mo[:, 32 * t:32 * t + 20], T.kys[:, 15:320:16], 1, -1280 + t, ["kys"], ["mo%d" % t])
+        lin(T.mo[:, 0:20], T.kys[:, 15:320:16], 0.25, -320, ["kys"], ["mo"])
         if rd == 1:
             for k, tgt in ((0, T.lrow), (1, T.rrow)):
                 cp(tgt[:], T.w4[:].indirect(T.lnu[:, 40 * k:40 * k + 40]), ["w4", "lnu"], ["row%d" % k], "av", n=640, x=True)
                 dma("s", [((T.ltb, T.rtb)[k][:], tgt[0:128:16, :])], ["row%d" % k], ["lr%d" % k], "dt%d" % k)
+                tab = (T.ltb, T.rtb)[k]
+                for c in (0, 1):
+                    lin(tab[:, c:40:2], tab[:, c:40:2], 0.25, -320, ["lr%d" % k], ["lr%d%s" % (k, "ab"[c])])
         if rd == 3:
             quant(T.vq[:], T.vs[:], T.vb[:], ["vb"], ["vq"])
         for h in (0, 1):
             lq, ls = T["lq%d" % rd], T["ls%d" % rd]
             for b in range(4):
-                mm(4 * h + b, 160, T.eq[:, 128 * b:128 * b + 128], T.es[:, 128 * b:128 * b + 128], lq[:, 160 * h:160 * h + 160], ls[:, 160 * h:160 * h + 160],
+                mm(4 * h + b, WID[h], T.eq[:, 128 * b:128 * b + 128], T.es[:, 128 * b:128 * b + 128], lq[:, cols(h)], ls[:, cols(h)],
                    ["eq", "lq%d%d" % (rd, h)])
             for b in range(4):
-                cp(T.dd[:, 640 * h + b:640 * h + 640:4], bank(4 * h + b, 160), ["b%d" % (4 * h + b)], ["dd%d%d" % (h, b)], "av", n=160)
+                cp(T.dd[:, 320 * b + AT[h]:320 * b + AT[h] + WID[h]], bank(4 * h + b, WID[h]), ["b%d" % (4 * h + b)], ["dd%d%d" % (h, b)], "av", n=WID[h])
         xn, qn, sn = T["x%d" % rd], T["qx%d" % rd], T["sx%d" % rd]
         for h in (0, 1):
             for t in range(4):
-                tt(xn[:, 640 * h + t:640 * h + 640:4], T.dd[:].indirect(T.mo[:, 32 * t + 10 * h:32 * t + 10 * h + 10]), T.vt[:, 640 * h + t:640 * h + 640:4], OP.add,
-                   ["mo%d" % t, "vt%d%d" % (h, t)] + ["@x"] * h + ["dd%d%d" % (i, b) for i in (0, 1) for b in range(4)], ["xn%d%d%d" % (rd, h, t)], n=160, x=True)
-            quant(qn[:, 160 * h:160 * h + 160], sn[:, 160 * h:160 * h + 160], xn[:, 640 * h:640 * h + 640], state_parts(rd, h), ["qx%d%d" % (rd, h)] + ["@x"] * (1 - h))
+                tt(xn[:, quad(h, t, 4)], T.dd[:, 320 * t:320 * t + 320].indirect(T.mo[:, part(h)]), T.vt[:, quad(h, t, 4)], OP.add,
+                   ["mo", "vt%d%d" % (h, t), "dd0%d" % t, "dd1%d" % t] + ["@x"] * h, ["xn%d%d%d" % (rd, h, t)], n=WID[h], x=True)
+            quant(qn[:, cols(h)], sn[:, cols(h)], xn[:, quad(h)], state_parts(rd, h), ["qx%d%d" % (rd, h)] + ["@x"] * (1 - h), 4 * WID[h])
             if rd == 3:
-                c = slice(160 * h, 160 * h + 160)
-                dma("s", [(T.oc[:, 640 * h:640 * h + 640], qn[:, c].bitcast(dt.uint8))] + [(T.osc[4 * k:4 * k + 4, c], sn[32 * k:32 * k + 4, c]) for k in range(4)],
+                c = cols(h)
+                dma("s", [(T.oc[:, quad(h)], qn[:, c].bitcast(dt.uint8))] + [(T.osc[4 * k:4 * k + 4, c], sn[32 * k:32 * k + 4, c]) for k in range(4)],
                     ["qx3%d" % h], [], "oq%d" % h)
             else:
                 scores(rd, h)
@@ -682,10 +705,9 @@ def rank_program(g, core, T, topo):
     mm(1, 320, T.vq[:], T.vs[:], T.qx3[:], T.sx3[:], ["vq", "qx30", "qx31"])
     cp(T.yb[:], bank(1, 320), ["b1"], ["yb"], "av", n=320)
     dma("s", [(T.y[:], T.yb[:])], ["yb"], [], "oy")
-    turn_tables()
-    for k, tab in enumerate((T.ltb, T.rtb)):
-        lin(T.lout[:, 40 * k:40 * k + 40], tab[:], 0.25, -320, ["lr%d" % k], ["lo%d" % k])
-        dma("s", [(T.lr[:, 640 * k:640 * k + 640], T.lout[:, 40 * k:40 * k + 40])], ["lo%d" % k], [], "ol")
+    turn_tables(True)
+    for k in (0, 1):
+        dma("s", [(T.lr[:, 640 * k:640 * k + 640], T.lout[:, 40 * k:40 * k + 40])], ["lo%da" % k, "lo%db" % k], [], "ol")
     issue()
     need("g", dict(total))
     g.wait_ge(T.sem.lsem, sent[0])

from concourse.bass import DstId, RemoteDMATransfer
from concourse.mybir import dt, AluOpType, ActivationFunctionType
import comms_topo

OP = AluOpType
AF = ActivationFunctionType
STEP = [4, 1, 2]
BIG = 1.0e6
WAKE, SPARE, LOOK = 0.07, 0.5, 0.3
EPS = 2.0 ** -93

F, B, I, U, C4, S8 = "float32", "bfloat16", "int32", "uint16", "float8_e4m3fn_x4", "uint8"
SCRATCH = {"ps": ("psum", [128, 4096], F)}
for _n, _w, _d in [
    ("x0", 1280, B), ("x1", 1280, B), ("x2", 1280, B), ("x3", 1280, B), ("xh", 1280, B), ("xg", 1280, B), ("vt", 1280, B), ("ht", 1280, B), ("dd", 1280, B),
    ("ub", 512, B), ("vb", 512, B), ("et", 2048, B), ("ones", 512, B),
    ("uq", 128, C4), ("us", 128, S8), ("vq", 128, C4), ("vs", 128, S8), ("wq", 512, C4), ("wsp", 512, S8),
    ("utq", 128, C4), ("uts", 128, S8), ("ufq", 768, C4), ("ufs", 768, S8), ("eq", 512, C4), ("es", 512, S8),
    ("qx0", 320, C4), ("sx0", 320, S8), ("qx1", 320, C4), ("sx1", 320, S8), ("qx2", 320, C4), ("sx2", 320, S8), ("qx3", 320, C4), ("sx3", 320, S8),
    ("qv", 320, C4), ("qvs", 320, S8),
    ("qh1", 320, C4), ("sh1", 320, S8), ("qh2", 320, C4), ("sh2", 320, S8), ("qh3", 320, C4), ("sh3", 320, S8),
    ("lq1", 320, C4), ("ls1", 320, S8), ("lq2", 320, C4), ("ls2", 320, S8), ("lq3", 320, C4), ("ls3", 320, S8), ("rlq", 320, C4), ("rls", 320, S8),
    ("nl", 320, I), ("nlu", 320, U), ("tw", 5120, F), ("tx", 3840, F), ("nw", 3840, B), ("w4", 320, F),
    ("cw", 120, F), ("cx", 120, F), ("fb", 60, F), ("fx", 120, F), ("fl", 240, F), ("flu", 256, U), ("lz", 64, F),
    ("jj", 320, I), ("jk", 320, I), ("mask", 320, F), ("rs", 320, F), ("rb", 800, F), ("st", 320, F),
    ("cid", 16, F), ("dva", 16, F), ("dvb", 16, F), ("ea", 16, F), ("da", 16, F), ("eb", 16, F), ("db", 16, F), ("tmp", 256, F),
    ("y1", 160, F), ("y1s", 160, F), ("y2i", 160, F), ("y2b", 160, F), ("y2", 960, F), ("y2s", 960, F), ("ye", 640, F), ("yes", 640, F),
    ("lu", 128, U), ("nu", 128, U), ("lt0", 16, F), ("lt1", 16, F), ("bc0", 320, B), ("bc1", 320, B), ("lw", 640, B), ("km", 320, B), ("kt", 320, B),
    ("mlu", 32, U), ("ld", 64, F), ("kl1", 20, U), ("kl2", 20, U), ("kl3", 20, U), ("kr1", 20, U), ("kr2", 20, U), ("kr3", 20, U), ("rlk", 20, U),
    ("kw", 320, F), ("ky", 320, F), ("kys", 320, F), ("mo", 128, U),
    ("sn", 320, F), ("fn", 20, F), ("ltb", 40, F), ("rtb", 40, F), ("lrow", 640, F), ("rrow", 640, F), ("lni", 80, I), ("lnu", 80, U), ("lout", 80, F), ("lt2", 64, F),
    ("yb", 320, F), ("sgc", 8, F), ("sgn", 8, F), ("cli", 64, I), ("clu", 64, U), ("ui", 64, I), ("uf", 64, F), ("uoff", 64, U), ("qi", 16, I), ("qf", 128, F),
]:
    SCRATCH[_n] = ("sbuf", [128, _w], _d)

SEMAPHORES = (["sv", "sa", "st", "sg", "dx0", "dx1", "du", "dv", "dw", "dl", "dt0", "dt1", "fn1", "fn2", "fn3", "oy", "ol", "oq0", "oq1", "dfx", "lsem", "ry0", "ry1", "rz0", "rz1", "rk"]
              + ["dn%d" % s for s in range(8)] + ["ar%d%d" % (r, h) for r in (1, 2, 3) for h in (0, 1)] + ["kr%d" % r for r in (1, 2, 3)])


AT, WID = (0, 160), (160, 160)


def cols(h):
    return slice(AT[h], AT[h] + WID[h])


def quad(h, t=0, step=1):
    return slice(4 * AT[h] + t, 4 * (AT[h] + WID[h]), step)


def part(h):
    return slice(AT[h] // 16, (AT[h] + WID[h]) // 16)


def bits_of(engines):
    m = 0
    for e in engines:
        m |= 1 << e
    return m


def relays_of(core, dst, topo):
    c = [k for k in topo.cores_of(core) if k != core and topo.may_write(k, dst)]
    return [[k for k in c if topo.die(k) == topo.die(core)][0], [k for k in c if topo.die(k) != topo.die(core)][0]]


def relay_program(g, core, T, topo):
    for r, src in enumerate(T.cores):
        dst = T.cores[r ^ STEP[1]]
        if core not in topo.cores_of(src) or core == src:
            continue
        rel = relays_of(src, dst, topo)
        if core not in rel:
            continue
        k = rel.index(core)
        rid, pid = topo.addr(dst, core)
        m, n = topo.mask(core, dst), len(topo.engines(core, dst))
        half = len(topo.engines(src, core)) // 2
        sent = 0
        if k == 0:
            g.wait_ge(T.sem.rk, half)
            g.remote_dma(T.kr2[:], T.rlk[:], T.sem.kr2, T.sem.lsem, pid, rid, m)
            sent += n
        for h in (0, 1):
            w = WID[h] // 2
            a = AT[h] + w * k
            g.wait_ge(T.sem["ry%d" % h], half)
            g.remote_dma(T.lq2[:, a:a + w].bitcast(dt.uint8), T.rlq[:, a:a + w].bitcast(dt.uint8), T.sem["ar2%d" % h], T.sem.lsem, pid, rid, m)
            g.wait_ge(T.sem["rz%d" % h], half)
            g.remote_dma(T.ls2[:, a:a + w], T.rls[:, a:a + w], T.sem["ar2%d" % h], T.sem.lsem, pid, rid, m)
            sent += 2 * n
        g.wait_ge(T.sem.lsem, sent)


def table_of(a, s):
    if s < 6:
        return ("l", s + 1) if s < 2 * a else ("r", 6 - s + 2 * a)
    return ("r", 7) if (s == 6) == (a == 0) else ("l", 0)


def rank_program(g, core, T, topo):
    rank = T.rank_of(core)
    if rank is None:
        relay_program(g, core, T, topo)
        return
    Q = {"g": g, "v": g.vector, "a": g.scalar, "t": g.tensor, "s": g.sync}
    SEM = {"g": "sg", "v": "sv", "a": "sa", "t": "st"}
    nodes, writer, readers = [], {}, {}

    def node(fns, cost, late, r, w, sem, inc):
        pre, after = set(), set()
        for k in list(r) + list(w):
            if k in writer:
                (after if k[0] == "@" else pre).add(writer[k])
        for k in w:
            if k[0] != "@":
                pre.update(readers.get(k, ()))
        i = len(nodes)
        nodes.append({"fns": fns, "cost": cost, "late": late, "pre": sorted(pre), "order": sorted(pre | after), "sem": sem, "inc": inc})
        for k in r:
            readers.setdefault(k, set()).add(i)
        for k in w:
            writer[k] = i
            readers[k] = set()

    def op(q, fn, r, w, us):
        node({q: fn}, {q: us}, 0.0, r, list(w) + (["gpsimd"] if q == "g" else []), None, 1)

    def dma(q, pairs, r, w, sem):
        def go(e):
            for o, i in pairs:
                e.dma_start(o, i).then_inc(T.sem[sem], 16)
        node({q: go}, {q: 0.06 * len(pairs)}, 2.0, r, w, sem, 16 * len(pairs))

    def us(n, cycles, gather):
        return 0.05 + n * 0.0015 if gather else max(64, n * cycles) * 0.001

    def tt(o, a, b, f, r, w, n=10, x=False, c=2):
        op("v", lambda e: e.tensor_tensor(o, a, b, f), r, w, us(n, c, x))

    def ts(o, a, s1, s2, f1, f2, r, w, n=10, x=False, c=1):
        if f2 is None:
            op("v", lambda e: e.tensor_scalar(o, a, s1, None, f1), r, w, us(n, c, x))
        else:
            op("v", lambda e: e.tensor_scalar(o, a, s1, s2, f1, f2), r, w, us(n, c, x))

    def lin(o, a, m, b, r, w, n=10, x=False):
        ts(o, a, float(m), float(b), OP.mult, OP.add, r, w, n, x)

    def cp(o, a, r, w, q="v", n=10, x=False, c=1):
        fns = {"v": lambda e: e.tensor_copy(o, a), "a": lambda e: e.activation(o, a, AF.Copy)}
        node({k: fns[k] for k in q}, {k: us(n, c if k == "v" else 1, x) for k in q}, 0.0, r, w, None, 1)

    def scaled(o, a, m, r, w, q, n, c=1):
        fns = {"v": lambda e: e.tensor_scalar(o, a, m, None, OP.mult), "a": lambda e: e.activation(o, a, AF.Copy, scale=m)}
        node({k: fns[k] for k in q}, {k: us(n, c if k == "v" else 1, False) for k in q}, 0.0, r, w, None, 1)

    def tr(o, a, r, w, n, c=1):
        op("v", lambda e: e.transpose(o, a), r, w, us(n, c, False))

    def scan(o, d0, d1, f0, f1, r, w, n=160):
        op("v", lambda e: e.tensor_tensor_scan(o, d0, d1, BIG, f0, f1), r, w, us(n, 1, False))

    def mm(bank, n, lq, lsc, rq, rsc, r):
        op("t", lambda e: e.matmul_mx(T.ps[:, 512 * bank:512 * bank + n], lq, lsc, rq, rsc, True, True), r, ["b%d" % bank], (n + 16) * 0.0011)

    def fill(o, c, w, n=10):
        op("v", lambda e: e.memset(o, c), [], w, us(n, 1, False))

    def quant(q, s, t, r, w, n=640):
        op("v", lambda e: e.quantize_mx(q, s, t), r, w, 0.012 + n * 0.00028)

    def arrange():
        n = len(nodes)
        tail = [0.0] * n
        out = [[] for _ in range(n)]
        for i, d in enumerate(nodes):
            for p in d["order"]:
                out[p].append(i)
        for i in range(n - 1, -1, -1):
            d = nodes[i]
            tail[i] = min(d["cost"].values()) + d["late"] + max([tail[k] + WAKE for k in out[i]] + [0.0])
        left = [len(d["order"]) for d in nodes]
        ready = [0.0] * n
        open_ = [i for i in range(n) if left[i] == 0]
        free, order = {}, []
        while open_:
            cand = []
            for i in open_:
                d = nodes[i]
                for q in d["cost"]:
                    s = max(free.get(q, 0.0), ready[i])
                    extra = SPARE if q == "v" and len(d["cost"]) > 1 else 0.0
                    cand.append((s, i, q, extra))
            best = {}
            for s, i, q, extra in cand:
                e = s + nodes[i]["cost"][q] + extra
                if i not in best or e < best[i][0]:
                    best[i] = (e, s, q)
            s0, i0 = min((v[1], i) for i, v in best.items())
            q0 = best[i0][2]
            same = [(i, v[1]) for i, v in best.items() if v[2] == q0]
            i = max([k for k in same if k[1] <= s0 + 1e-9], key=lambda k: tail[k[0]])[0]
            c = nodes[i]["cost"][q0]
            soon = [k for k in same if k[1] < s0 + LOOK * c and tail[k[0]] > tail[i]]
            if soon:
                i = max(soon, key=lambda k: tail[k[0]])[0]
            e, s, q = best[i]
            open_.remove(i)
            free[q] = s + nodes[i]["cost"][q]
            order.append((s, len(order), i, q))
            for k in out[i]:
                left[k] -= 1
                ready[k] = max(ready[k], free[q] + nodes[i]["late"] + WAKE)
                if left[k] == 0:
                    open_.append(k)
        return [(i, q) for s, m, i, q in order]

    total, waited = {}, {}

    def need(q, deps):
        for sem in sorted(deps):
            if waited.get((q, sem), 0) < deps[sem]:
                waited[(q, sem)] = deps[sem]
                Q[q].wait_ge(T.sem[sem], deps[sem])

    def issue():
        done = {}
        for i, q in arrange():
            d = nodes[i]
            deps = {}
            for p in d["pre"]:
                sem, v = done[p]
                deps[sem] = max(deps.get(sem, 0), v)
            need(q, deps)
            inst = d["fns"][q](Q[q])
            sem = d["sem"] or SEM[q]
            if d["sem"] is None:
                inst.then_inc(T.sem[sem], 1)
            total[sem] = total.get(sem, 0) + d["inc"]
            done[i] = (sem, total[sem])

    def bank(b, n):
        return T.ps[:, 512 * b:512 * b + n]

    mask1, rst1 = T.mask[:, 0:160], T.rs[:, 0:160]

    for h in (0, 1):
        dma("s", [(T.x0[:, quad(h)], T.x[:, quad(h)])], [], ["x0%d" % h], "dx%d" % h)
    dma("a", [(T.ub[:], T.u[:])], [], ["ub"], "du")
    for k, s in enumerate((6, 0, 7, 1, 2, 3, 4, 5)):
        pairs = []
        for a in range(4):
            side, gr = table_of(a, s)
            src = (T.lam if side == "l" else T.rho)[16 * gr:16 * gr + 16, :]
            for b in (0, 1):
                p = 16 * (2 * a + b)
                pairs.append((T.nl[p:p + 16, 40 * s:40 * s + 40], src))
        dma("s" if k % 2 == 0 else "a", pairs, [], ["nl%d" % s], "dn%d" % s)
    dma("s", [(T.wq[:].bitcast(dt.uint8), T.wc[:]), (T.wsp[:], T.ws[:])], [], ["wq"], "dw")
    dma("s", [(T.lni[:, 0:40], T.lam[:]), (T.lni[:, 40:80], T.rho[:])], [], ["lni"], "dl")
    dma("s", [(T.vb[:], T.v[:])], [], ["vb"], "dv")

    def iota(o, pattern, base, cm, w, fl=False):
        n = 1
        for step, count in pattern:
            n *= count
        if fl:
            op("g", lambda e: e.iota(o, pattern, base, cm, allow_small_or_imprecise_dtypes=True), [], w, 0.15 + 0.002 * n)
        else:
            op("g", lambda e: e.iota(o, pattern, base, cm), [], w, 0.15 + 0.002 * n)

    iota(T.qi[:, 0:4], [[0, 4]], 0, 1, ["qi"])
    iota(T.uf[:, 0:4], [[2, 4]], 0, 0, ["ufa"], True)
    iota(T.uf[:, 4:8], [[32, 4]], 96, 0, ["ufb"], True)
    iota(T.ui[:, 0:48], [[-16, 6], [32, 4], [0, 2]], 97, 0, ["ui"])
    iota(T.w4[:], [[4, 320]], 1280, 0, ["w4"], True)
    iota(T.jj[:], [[1, 320]], 128, -1, ["jj"])
    iota(T.jk[:], [[1, 320]], 0, 0, ["jk"])
    for a in range(4):
        iota(T.cid[32 * a:32 * a + 32, 0:10], [[128, 10]], 1280, 4, ["cid%d" % a], True)
    CID = ["cid%d" % a for a in range(4)]
    iota(T.cli[:, 0:10], [[1, 10]], 0, 0, ["cl16"])
    iota(T.cli[:, 32:52], [[1, 10], [0, 2]], 0, 0, ["cl32"])

    ts(T.qi[:, 4:8], T.qi[:, 0:4], 15, None, OP.bitwise_and, None, ["qi"], ["qa"])
    q4 = T.qf[:, 0:4]
    cp(q4, T.qi[:, 4:8], ["qa"], ["q4"])
    qe = T.qf[:, 20:24]
    ts(T.qf[:, 24:28], q4, 10.0, -10.0, OP.is_ge, OP.mult, ["q4"], ["q_t"])
    tt(qe, q4, T.qf[:, 24:28], OP.add, ["q4", "q_t"], ["qe"])
    tt(T.qf[:, 4:8], qe, T.uf[:, 0:4], OP.is_lt, ["qe", "ufa"], ["q_m"])
    ts(T.qf[:, 8:12], qe, -16.0, None, OP.mult, None, ["qe"], ["q_r"])
    tt(T.qf[:, 8:12], T.qf[:, 8:12], T.uf[:, 4:8], OP.add, ["q_r", "ufb"], ["q_r"])
    lin(T.qf[:, 12:16], qe, 16, 16, ["qe"], ["q_l"])
    tt(T.qf[:, 12:16], T.qf[:, 12:16], T.qf[:, 8:12], OP.subtract, ["q_l", "q_r"], ["q_l"])
    tt(T.qf[:, 12:16], T.qf[:, 12:16], T.qf[:, 4:8], OP.mult, ["q_l", "q_m"], ["q_l"])
    tt(T.qf[:, 8:12], T.qf[:, 8:12], T.qf[:, 12:16], OP.add, ["q_r", "q_l"], ["q_r"])
    ts(T.qf[:, 16:20], qe, 6.0, None, OP.is_lt, None, ["qe"], ["q_6"])
    tt(T.qf[:, 8:12], T.qf[:, 8:12], T.qf[:, 16:20], OP.mult, ["q_r", "q_6"], ["q_r"])
    ts(T.qf[:, 28:32], q4, 10.0, None, OP.is_ge, None, ["q4"], ["q_10"])
    tt(T.qf[:, 8:12], T.qf[:, 8:12], T.qf[:, 28:32], OP.add, ["q_r", "q_10"], ["q_r"])
    for k, (c, spec) in enumerate(((4, ((7, 112.0), (8, 1.0), (9, 113.0))), (1, ((6, 112.0), (8, 113.0), (9, 1.0))))):
        o = 32 + 32 * k
        for j, (q, val) in enumerate(spec):
            ts(T.qf[:, o + 4 * j:o + 4 * j + c], T.qf[:, 0:c], float(q), val, OP.is_equal, OP.mult, ["q4"], ["qs%d%d" % (k, j)])
        tt(T.qf[:, o:o + c], T.qf[:, o:o + c], T.qf[:, o + 4:o + 4 + c], OP.add, ["qs%d0" % k, "qs%d1" % k], ["qs%d0" % k])
        tt(T.qf[:, o:o + c], T.qf[:, o:o + c], T.qf[:, o + 8:o + 8 + c], OP.add, ["qs%d0" % k, "qs%d2" % k], ["qs%d0" % k])
    cp(T.qf[:, 32:33], T.qf[:, 64:65], ["qs10", "qs00"], ["qs00"])
    tt(T.qf[:, 8:12], T.qf[:, 8:12], T.qf[:, 32:36], OP.add, ["q_r", "qs00"], ["q_r"])
    cp(T.uoff[:, 0:8:2], T.qf[:, 8:12], ["q_r"], ["uoff0"])
    cp(T.uoff[:, 1:8:2], T.qf[:, 8:12], ["q_r"], ["uoff1"])
    quant(T.uq[:, 0:128], T.us[:, 0:128], T.ub[:, 0:512], ["ub"], ["uq"])
    cp(T.utq[:, 0:128].bitcast(dt.uint32), T.uq[:, 0:128].bitcast(dt.uint32).indirect(T.uoff[:, 0:8]), ["uq", "uoff0", "uoff1"], ["utq"], n=128, x=True)
    cp(T.uts[:, 0:128], T.us[:, 0:128].indirect(T.uoff[:, 0:8]), ["uq", "uoff0", "uoff1"], ["uts"], "av", n=128, x=True)

    ts(T.jj[:], T.jj[:], 15, None, OP.bitwise_and, None, ["jj"], ["jj"], n=320)
    ts(T.mask[:], T.jj[:], 0.0, None, OP.is_equal, None, ["jj"], ["mask"], n=320)
    ts(T.jk[:], T.jk[:], 15, None, OP.bitwise_and, None, ["jk"], ["jk"], n=320)
    ts(T.rs[:], T.jk[:], 0.0, BIG, OP.is_gt, OP.mult, ["jk"], ["rs"], n=320)

    def list_of(s):
        cp(T.nlu[:, 40 * s:40 * s + 40], T.nl[:, 40 * s:40 * s + 40], ["nl%d" % s], ["nlu%d" % s])

    def window(s):
        cp(T.tw[:, 640 * s:640 * s + 640], T.w4[:].indirect(T.nlu[:, 40 * s:40 * s + 40]), ["w4", "nlu%d" % s], ["tw%d" % s], "av", n=640, x=True)

    for s in (6, 0, 7, 1, 2, 3, 4, 5):
        list_of(s)
        window(s)
    iota(T.cw[:], [[0, 6], [32, 20]], 0, 0, ["cw"], True)
    ts(T.qf[:, 96:97], T.qf[:, 0:1], 2.0, None, OP.mult, None, ["q4"], ["q2"])
    ts(T.cw[:], T.cw[:], T.qf[:, 96:97], None, OP.add, None, ["cw", "q2"], ["cw"], n=120)
    lin(T.cx[:], T.cw[:], 1, 1, ["cw"], ["cx"], n=120)
    for h in (0, 1):
        quant(T.qx0[:, cols(h)], T.sx0[:, cols(h)], T.x0[:, quad(h)], ["x0%d" % h], ["qx0%d" % h], 4 * WID[h])
    for k in range(3):
        w = 320 if k < 2 else 160
        cp(T.rb[:, 320 * k:320 * k + w], T.rs[:, 0:w], ["rs"], ["rb%d" % s for s in ((1, 2), (3, 4), (5,))[k]], "av", n=w)
    cp(T.clu[:, 0:10], T.cli[:, 0:10], ["cl16"], ["c16"])
    cp(T.clu[:, 32:52], T.cli[:, 32:52], ["cl32"], ["c32"])
    cp(T.lt0[0:32, 0:10], T.cid[0:32, 0:10], CID, ["lt0_0"])
    cp(T.lt1[96:128, 0:10], T.cid[96:128, 0:10], CID, ["lt1_3"])
    fill(T.ones[:], 1.0, ["ones"], n=256)

    def one_in(b):
        op("g", lambda e: e.affine_select(T.et[:, 512 * b:512 * b + 512], T.ones[:], [[1, 512]], OP.is_equal, 0.0, -b, -4), ["ones"], ["et%d" % b], 1.2)

    for b in range(4):
        one_in(b)

    def half_x(k, h):
        x = T["x%d" % k]
        for t in range(4):
            scaled(T.xh[:, 320 * t + AT[h]:320 * t + AT[h] + WID[h]], x[:, quad(h, t, 4)], 0.5, state_parts(k, h)[t % len(state_parts(k, h)):][:1],
                   ["xh%d%d" % (h, t)], "av", WID[h], 0.5)
        scaled(T.xg[:, quad(h)], x[:, quad(h)], 0.5, state_parts(k, h), ["xg%d" % h], "av", 4 * WID[h], 0.5)

    def state_parts(k, h):
        return ["x0%d" % h] if k == 0 else ["xn%d%d%d" % (k, h, t) for t in range(4)]

    half_x(0, 0)
    half_x(0, 1)

    def scores(k, h):
        mm(h, WID[h], T.utq[:], T.uts[:], T["qx%d" % k][:, cols(h)], T["sx%d" % k][:, cols(h)], ["utq", "uts", "qx%d%d" % (k, h)])
        tr(T.st[:, cols(h)], bank(h, WID[h]), ["b%d" % h], ["st%d" % h], WID[h])

    ST = ["st0", "st1"]

    def row(q):
        return T.st[:, q:320:32]

    def tmp(k):
        return T.tmp[:, 16 * k:16 * k + 10]

    def rstart(s):
        return T.rb[:, 160 * (s - 1):160 * s:16]

    def sign(s, j):
        o, i, sg = T.nw[:, 640 * s + 320 * j:640 * s + 320 * j + 320], bank(2 + s, 320), (T.sgn, T.sgc)[j][:, s:s + 1]
        eps = EPS if j else -EPS
        op("a", lambda e: e.activation(o, i, AF.Sign, bias=eps, scale=sg), ["b%d" % (2 + s), "sgc"], ["nw%d%d" % (s, j)], 0.33)

    def flips(k):
        for s in range(6):
            mm(2 + s, 320, T.ufq[:, 128 * s:128 * s + 128], T.ufs[:, 128 * s:128 * s + 128], T["qx%d" % k][:], T["sx%d" % k][:], ["ufq", "ufs", "qx%d0" % k, "qx%d1" % k])
        for s in range(6):
            sign(s, 0)
            sign(s, 1)

    def turn_windows():
        for s in range(6):
            ts(T.fb[:, 10 * s:10 * s + 10], row(10 + s), T.sgc[:, s:s + 1], 0.0, OP.mult, OP.is_lt, ST + ["sgc"], ["fb%d" % s])
        pairs = []
        for a in range(4):
            for b in (0, 1):
                for c in (0, 1):
                    p, q = 32 * a + 16 * b, 32 * a + 16 * c
                    pairs.append((T.fx[q:q + 16, 60 * b:60 * b + 60], T.fb[p:p + 16, :]))
        dma("s", pairs, ["fb%d" % s for s in range(6)], ["fx"], "dfx")
        for k, (base, f) in enumerate(((T.cw, OP.add), (T.cx, OP.subtract))):
            for b in (0, 1):
                tt(T.fl[:, 120 * k + b:120 * k + 120:2], base[:, b:120:2], T.fx[:, 60 * b:60 * b + 60], f, ["fx", "cw", "cx"], ["fl%d%d" % (k, b)], n=60)
            cp(T.flu[:, 128 * k:128 * k + 120], T.fl[:, 120 * k:120 * k + 120], ["fl%d0" % k, "fl%d1" % k], ["flu%d" % k], n=120)
        for s in range(6):
            for k in (0, 1):
                cp(T.tx[:, 640 * s + k:640 * s + 640:2], T.tw[:, 640 * s:640 * s + 640].indirect(T.flu[:, 128 * k + 20 * s:128 * k + 20 * s + 20]),
                   ["flu%d" % k, "tw%d" % s], ["tx%d%d" % (s, k)], "av", n=320, x=True)

    def direct(n, rd):
        dv = (T.dva, T.dvb)[n][:, 0:10]
        name = ("dva", "dvb")[n]
        o = 5 * n
        if rd == 1:
            ts(tmp(o), row(6 + n), 0.0, 2.0, OP.is_gt, OP.mult, ST, ["t%d" % o])
            tt(tmp(o), tmp(o), T.cid[:, 0:10], OP.add, ["t%d" % o] + CID, ["t%d" % o])
            lin(T.nu[:, 96 + 16 * n:106 + 16 * n], tmp(o), 0.5, -640, ["t%d" % o], ["nu%d" % (6 + n)])
            tt(T.ye[:, 160 * n:160 * n + 160], T.tw[:, 640 * (6 + n):640 * (7 + n)].indirect(T.nu[:, 96 + 16 * n:106 + 16 * n]), mask1, OP.mult,
               ["tw%d" % (6 + n), "nu%d" % (6 + n), "mask"], ["ye%d" % n], n=160, x=True)
            scan(T.yes[:, 160 * n:160 * n + 160], rst1, T.ye[:, 160 * n:160 * n + 160], OP.min, OP.add, ["rs", "ye%d" % n], ["yes%d" % n])
            cp(dv, T.yes[:, 160 * n + 15:160 * n + 160:16], ["yes%d" % n], [name])
        else:
            e, d = (T.ea, T.eb)[n][:, 0:10], (T.da, T.db)[n][:, 0:10]
            ts(tmp(o), row(6 + n), 0.0, None, OP.is_gt, None, ST, ["t%d" % o])
            ts(tmp(o + 1), row(8 + n), T.sgc[:, 6 + n:7 + n], 0.0, OP.mult, OP.is_lt, ST + ["sgc"], ["t%d" % (o + 1)])
            tt(tmp(o + 2), tmp(o), tmp(o + 1), OP.not_equal, ["t%d" % o, "t%d" % (o + 1)], ["t%d" % (o + 2)])
            tt(tmp(o + 2), tmp(o + 2), d, OP.mult, ["t%d" % (o + 2), "d%d" % n], ["t%d" % (o + 2)])
            tt(dv, e, tmp(o + 2), OP.add, ["e%d" % n, "t%d" % (o + 2)], [name])

    def turn_direct(n):
        o = 5 * n
        e, d = (T.ea, T.eb)[n][:, 0:10], (T.da, T.db)[n][:, 0:10]
        tt(tmp(o + 3), tmp(o + 1), d, OP.mult, ["t%d" % (o + 1), "d%d" % n], ["t%d" % (o + 3)])
        tt(e, e, tmp(o + 3), OP.add, ["e%d" % n, "t%d" % (o + 3)], ["e%d" % n])
        tt(d, d, tmp(o + 3), OP.subtract, ["d%d" % n, "t%d" % (o + 3)], ["d%d" % n])
        tt(d, d, tmp(o + 3), OP.subtract, ["d%d" % n, "t%d" % (o + 3)], ["d%d" % n])

    def spread(j):
        o, win, lst = (T.bc0, T.bc1)[j][:], (T.lt0, T.lt1)[j][:, 0:10], T.clu[:, 32:52]
        node({"v": lambda e: e.tensor_scalar(o, win.indirect(lst), 0.25, -480.0, OP.mult, OP.add),
              "a": lambda e: e.activation(o, win.indirect(lst), AF.Copy, bias=-480.0, scale=0.25)},
             {"v": us(320, 1, True), "a": us(320, 1, True)}, 0.0, ["c32"] + ["lt%d_%d" % (j, a) for a in range(4)], ["bc%d" % j], None, 1)
        tr(T.lw[:, 320 * j:320 * j + 320], o, ["bc%d" % j], ["lw%d" % j], 320, 0.5)

    def lu(s):
        return T.lu[:, 16 * s:16 * s + 10]

    def walk(rd):
        fl = rd > 1
        rsc, cm, cb = (1280.0, 0.25, -320) if fl else (2.0, 0.5, -640)

        def bits(s):
            ts(rstart(s), row(s), 0.0, rsc, OP.is_gt, OP.mult, ST, ["rb%d" % s])

        direct(0, rd)
        ts(tmp(10), row(0), 0.0, rsc, OP.is_gt, OP.mult, ST, ["t10"])
        tt(tmp(10), tmp(10), T.dva[:, 0:10], OP.add, ["t10", "dva"], ["t10"])
        lin(lu(0), tmp(10), cm, cb, ["t10"], ["lu0a"])
        if fl:
            tt(T.y2i[:], T.dva[:, 0:10].indirect(T.clu[:, 0:10]), mask1, OP.mult, ["dva", "c16", "mask"], ["y2i"], n=160, x=True)
        tabs = T.tx if rd == 3 else T.tw
        for s in range(6):
            L = ["lu%d%s" % (s, c) for c in "abc"]
            prev = "y2i" if s == 0 else "y2%d" % (s - 1)
            if fl:
                pv = T.y2i[:] if s == 0 else T.y2[:, 160 * (s - 1):160 * s]
                tt(T.y1[:], T.nw[:, 640 * s:640 * s + 640].indirect(lu(s)), pv, OP.add, L + ["nw%d0" % s, "nw%d1" % s, prev, prev + "x"], ["y1"], n=160, x=True)
            if s < 5:
                bits(s + 1)
            if fl:
                scan(T.y1s[:], rst1, T.y1[:], OP.min, OP.max, ["rs", "y1"], ["y1s"])
                nu = T.nu[:, 16 * s:16 * s + 10]
                lin(nu, T.y1s[:, 15:160:16], 0.5, -639.5, ["y1s"], ["nu%d" % s])
                L, lst = ["nu%d" % s], nu
            else:
                lst = lu(s)
            y2, y2s = T.y2[:, 160 * s:160 * s + 160], T.y2s[:, 160 * s:160 * s + 160]
            tt(y2, tabs[:, 640 * s:640 * s + 640].indirect(lst), mask1, OP.mult, L + (["tx%d0" % s, "tx%d1" % s] if rd == 3 else ["tw%d" % s]) + ["mask"],
               ["y2%d" % s, "y2%dx" % s], n=160, x=True)
            rs = T.rb[:, 160 * s:160 * s + 160] if s < 5 else rst1
            scan(y2s, rs, y2, OP.min, OP.add, ["y2%d" % s, "y2%dx" % s, "rb%d" % (s + 1), "rs"], ["y2s%d" % s])

            def last(lo, hi):
                return T.y2s[lo:hi, 160 * s + 15:160 * s + 160:16]

            def rst(lo, hi):
                return T.rb[lo:hi, 160 * s:160 * s + 160:16]

            if s < 5:
                n = 16 * (s + 1)
                for k, (lo, hi) in enumerate({1: ((0, 32), (64, 128)), 3: ((0, 64), (96, 128))}.get(s, ((0, 128),))):
                    lin(T.lu[lo:hi, n:n + 10], last(lo, hi), cm, cb, ["y2s%d" % s], ["lu%d%s" % (s + 1, "ab"[k])])
            if s in (1, 3) and fl:
                lo = 32 if s == 1 else 64
                cp(T.y2[lo:lo + 32, 160 * s:160 * s + 160], T.y2b[lo:lo + 32, :], ["y2b", "y2%d" % s], ["y2%dx" % s], n=160)
            lo = 32 * (1 + s // 2)
            lt = (T.lt0, T.lt1)[s % 2]
            if s < 5:
                tt(lt[lo:lo + 32, 0:10], last(lo, lo + 32), rst(lo, lo + 32), OP.subtract, ["y2s%d" % s, "rb%d" % (s + 1)], ["lt%d_%d" % (s % 2, lo // 32)])
            if s == 0:
                direct(1, rd)
                cp(T.lt1[0:32, 0:10], T.dvb[0:32, 0:10], ["dvb"], ["lt1_0"])
                lin(T.mlu[96:128, 0:20:2], T.dvb[96:128, 0:10], 0.25, -320, ["dvb"], ["ml_e3"])
                if fl:
                    tt(T.y2b[:], T.dvb[:, 0:10].indirect(T.clu[:, 0:10]), mask1, OP.mult, ["dvb", "c16", "mask"], ["y2b"], n=160, x=True)
            if s in (0, 2):
                k = s + 2
                lo = 16 * k
                if k == 2:
                    ts(tmp(11), row(2), 0.0, rsc, OP.is_gt, OP.mult, ST, ["t11"])
                else:
                    ts(tmp(11), row(4), 0.0, rsc, OP.is_gt, OP.mult, ST, ["t11"])
                tt(tmp(11), tmp(11), T.dvb[:, 0:10], OP.add, ["t11", "dvb"], ["t11"])
                lin(T.lu[lo:lo + 32, 16 * k:16 * k + 10], T.tmp[lo:lo + 32, 176:186], cm, cb, ["t11"], ["lu%dc" % k])
            if s == 4:
                tt(T.tmp[0:96, 192:202], last(0, 96), rst(0, 96), OP.subtract, ["y2s4", "rb5"], ["t12"])
                ts(T.mlu[0:96, 1:20:2], T.tmp[0:96, 192:202], 0.25, None, OP.mult, None, ["t12"], ["ml_o"])
            if s in (3, 4):
                spread(4 - s)
            if s == 5:
                ts(T.mlu[96:128, 1:20:2], last(96, 128), 0.25, None, OP.mult, None, ["y2s5"], ["ml_o3"])
                lin(T.mlu[0:96, 0:20:2], last(0, 96), 0.25, -320, ["y2s5"], ["ml_e"])
        cp(T.km[:], T.lw[:].indirect(T.mlu[:, 0:20]), ["lw0", "lw1", "ml_e", "ml_o", "ml_e3", "ml_o3"], ["km"], n=320, x=True)
        tr(T.kt[:], T.km[:], ["km"], ["kt"], 320, 0.5)
        lin(T["kl%d" % rd][:], T.kt[:, 0:320:16], 1, 160, ["kt"], ["kl%d" % rd])

    sent = [0]

    def send(rd, what, h):
        dst = T.cores[rank ^ STEP[rd - 1]]
        def put(fn, cost, late, land, sem, inc, own):
            sent[0] += own
            node({"g": fn}, {"g": cost}, late, ["kl%d" % rd if what == "k" else "qh%d%d" % (rd, h)], [land], sem, inc)

        q, s, lq, ls = T["qh%d" % rd], T["sh%d" % rd], T["lq%d" % rd], T["ls%d" % rd]
        if topo.may_write(core, dst):
            rid, pid = topo.addr(dst, core)
            m, n = topo.mask(core, dst), len(topo.engines(core, dst))
            if what == "k":
                put(lambda e: e.remote_dma(T["kr%d" % rd][:], T["kl%d" % rd][:], T.sem["kr%d" % rd], T.sem.lsem, pid, rid, m), 1.0, 2.5, "kr%d" % rd, "kr%d" % rd, n, n)
                return
            c = cols(h)
            sem = T.sem["ar%d%d" % (rd, h)]

            def go(e):
                e.remote_dma(lq[:, c].bitcast(dt.uint8), q[:, c].bitcast(dt.uint8), sem, T.sem.lsem, pid, rid, m)
                e.remote_dma(ls[:, c], s[:, c], sem, T.sem.lsem, pid, rid, m)

            put(go, 2.0, 4.0, "lq%d%d" % (rd, h), "ar%d%d" % (rd, h), 2 * n, 2 * n)
            return
        rel = relays_of(core, dst, topo)
        ways = [topo.addr(k, core) for k in rel]
        eng = topo.engines(core, rel[0])
        n = len(eng) // 2
        masks = [bits_of(eng[:n]), bits_of(eng[n:])]
        far = len(topo.engines(rel[0], dst))
        if what == "k":
            put(lambda e: e.remote_dma(T.rlk[:], T["kl%d" % rd][:], T.sem.rk, T.sem.lsem, ways[0][1], ways[0][0], masks[0]), 1.0, 5.0, "kr%d" % rd, "kr%d" % rd, far, n)
            return

        w = WID[h] // 2

        def both_ways(e, view, land, sem):
            tr_ = []
            for k in (0, 1):
                a = AT[h] + w * k
                tr_.append(RemoteDMATransfer(dst_ids=[DstId(rid=ways[k][0], pnc=ways[k][1])], dma_engine_mask=masks[k], remote_sem=sem,
                                             src=view(a), dst=land(a)))
            e.remote_dma_fused(tr_, local_sem=T.sem.lsem)

        def go2(e):
            both_ways(e, lambda a: q[:, a:a + w].bitcast(dt.uint8), lambda a: T.rlq[:, a:a + w].bitcast(dt.uint8), T.sem["ry%d" % h])
            both_ways(e, lambda a: s[:, a:a + w], lambda a: T.rls[:, a:a + w], T.sem["rz%d" % h])

        put(go2, 2.0, 6.0, "lq%d%d" % (rd, h), "ar%d%d" % (rd, h), 4 * far, 4 * n)

    def meet(rd, h):
        for t in range(4):
            tt(T.vt[:, quad(h, t, 4)], T.xh[:, 320 * t:320 * t + 320].indirect(T["kl%d" % rd][:, part(h)]), T.xg[:, quad(h, t, 4)], OP.add,
               ["xh0%d" % t, "xh1%d" % t, "xg%d" % h, "kl%d" % rd] + ["@v"] * h, ["vt%d%d" % (h, t)], n=WID[h], x=True)

    def layer(h):
        c = cols(h)
        for b in range(4):
            mm(4 * h + b, WID[h], T.wq[:, 128 * b:128 * b + 128], T.wsp[:, 128 * b:128 * b + 128], T.qv[:, c], T.qvs[:, c], ["wq", "qv%d" % h])

    def layer_out(h, b, q):
        scaled(T.ht[:, quad(h, b, 4)], bank(4 * h + b, WID[h]), 0.03125, ["b%d" % (4 * h + b)], ["ht%d%d" % (h, b)], q, WID[h])

    def quant_v(h):
        quant(T.qv[:, cols(h)], T.qvs[:, cols(h)], T.vt[:, quad(h)], ["vt%d%d" % (h, t) for t in range(4)], ["qv%d" % h] + ["@v"] * (1 - h), 4 * WID[h])

    def quant_h(rd, h):
        quant(T["qh%d" % rd][:, cols(h)], T["sh%d" % rd][:, cols(h)], T.ht[:, quad(h)], ["ht%d%d" % (h, b) for b in range(4)], ["qh%d%d" % (rd, h)], 4 * WID[h])

    def natural(k, rd):
        mm(0, 320, T.uq[:], T.us[:], T["qx%d" % k][:], T["sx%d" % k][:], ["uq", "qx%d0" % k, "qx%d1" % k])
        cp(T.sn[:], bank(0, 320), ["b0"], ["sn"], "av", n=320)
        dma("s", [(T.fn[:], T.sn[1:128:16, :])], ["sn"], ["fn"], "fn%d" % rd)

    def turn_tables(final=False):
        for k, (tab, f) in enumerate(((T.ltb, OP.is_lt), (T.rtb, OP.is_gt))):
            n = "lr%d" % k
            a, d, z = T.lt2[:, 32 * k:32 * k + 20], T.ld[:, 32 * k:32 * k + 20], T.lz[:, 32 * k:32 * k + 20]
            e0, e1 = tab[:, 0:40:2], tab[:, 1:40:2]
            o = T.lout[:, 40 * k:40 * k + 40] if final else tab
            tt(d, e1, e0, OP.subtract, [n + "a", n + "b"], [n + "d"])
            ts(a, T.fn[:], 0.0, None, f, None, ["fn"], [n + "t"])
            tt(z, d, a, OP.mult, [n + "d", n + "t"], [n + "z"])
            tt(o[:, 0:40:2], e0, z, OP.add, [n + "a", n + "z"], [("lo%da" % k) if final else n + "a"])
            tt(o[:, 1:40:2], e1, z, OP.subtract, [n + "b", n + "z"], [("lo%db" % k) if final else n + "b"])

    for h in (0, 1):
        scores(0, h)
    for rd in (1, 2, 3):
        walk(rd)
        send(rd, "k", 0)
        meet(rd, 0)
        quant_v(0)
        layer(0)
        for b in range(4):
            layer_out(0, b, "av")
        meet(rd, 1)
        quant_v(1)
        layer(1)
        quant_h(rd, 0)
        send(rd, "h", 0)
        for b in range(4):
            layer_out(1, b, "av")
        quant_h(rd, 1)
        send(rd, "h", 1)
        if rd == 1:
            quant(T.eq[:], T.es[:], T.et[:], ["et%d" % b for b in range(4)], ["eq"], n=2048)
            for s in range(6):
                fill(T.ui[:, 8 * s + 2 * (s // 2 + 1):8 * s + 8], 16 * (s + 1) + 1, ["ui"])
            cp(T.uoff[:, 8:56], T.ui[:, 0:48], ["ui"], ["uoff2"])
            fill(T.sgc[:], 1.0, ["sgc"])
            for hi, lo in ((32, 0), (64, 2), (96, 4)):
                fill(T.sgc[0:hi, lo:6], -1.0, ["sgc"])
            fill(T.sgc[0:32, 6:7], -1.0, ["sgc"])
            fill(T.sgc[32:64, 7:8], -1.0, ["sgc"])
            fill(T.sgc[64:128, 7:8], -1.0, ["sgc"])
            ts(T.sgn[:], T.sgc[:], -1.0, None, OP.mult, None, ["sgc"], ["sgc"])
            cp(T.ufq[:].bitcast(dt.uint32), T.uq[:, 0:128].bitcast(dt.uint32).indirect(T.uoff[:, 8:56]), ["uq", "uoff2"], ["ufq"], n=768, x=True)
            cp(T.ufs[:], T.us[:, 0:128].indirect(T.uoff[:, 8:56]), ["uq", "uoff2"], ["ufs"], "av", n=768, x=True)
            for n in (0, 1):
                for c in (0, 1):
                    k = 2 * n + c
                    if n == 0:
                        lin(T.lu[:, 96 + 16 * c:106 + 16 * c], T.cid[:, 0:10], 0.5, -640 + c, CID, ["lc%d" % c])
                    tt(T.ye[:, 160 * k:160 * k + 160], T.tw[:, 640 * (6 + n):640 * (7 + n)].indirect(T.lu[:, 96 + 16 * c:106 + 16 * c]), mask1, OP.mult,
                       ["tw%d" % (6 + n), "lc%d" % c, "mask"], ["ye%d" % k], n=160, x=True)
                    scan(T.yes[:, 160 * k:160 * k + 160], rst1, T.ye[:, 160 * k:160 * k + 160], OP.min, OP.add, ["rs", "ye%d" % k], ["yes%d" % k])
                e, d = (T.ea, T.eb)[n][:, 0:10], (T.da, T.db)[n][:, 0:10]
                first, second = T.yes[:, 320 * n + 15:320 * n + 160:16], T.yes[:, 320 * n + 175:320 * n + 320:16]
                cp(e, first, ["yes%d" % (2 * n)], ["e%d" % n])
                tt(d, second, first, OP.subtract, ["yes%d" % (2 * n), "yes%d" % (2 * n + 1)], ["d%d" % n])
            cp(T.lnu[:], T.lni[:], ["lni"], ["lnu"], n=80)
        elif rd == 2:
            turn_direct(0)
            turn_direct(1)
        kl, kr = T["kl%d" % rd], T["kr%d" % rd]
        cp(T.kw[:], T.w4[:].indirect(kr[:]), ["w4", "kr%d" % rd], ["kw"], "av", n=320, x=True)
        tt(T.ky[:], T.kw[:].indirect(kl[:]), T.mask[:], OP.mult, ["kw", "kl%d" % rd, "mask"], ["ky"], n=320, x=True)
        scan(T.kys[:], T.rs[:], T.ky[:], OP.min, OP.add, ["ky", "rs"], ["kys"], n=320)
        lin(T.mo[:, 0:20], T.kys[:, 15:320:16], 0.25, -320, ["kys"], ["mo"])
        if rd == 1:
            for k, tgt in ((0, T.lrow), (1, T.rrow)):
                cp(tgt[:], T.w4[:].indirect(T.lnu[:, 40 * k:40 * k + 40]), ["w4", "lnu"], ["row%d" % k], "av", n=640, x=True)
                dma("s", [((T.ltb, T.rtb)[k][:], tgt[0:128:16, :])], ["row%d" % k], ["lr%d" % k], "dt%d" % k)
                tab = (T.ltb, T.rtb)[k]
                for c in (0, 1):
                    lin(tab[:, c:40:2], tab[:, c:40:2], 0.25, -320, ["lr%d" % k], ["lr%d%s" % (k, "ab"[c])])
        if rd == 3:
            quant(T.vq[:], T.vs[:], T.vb[:], ["vb"], ["vq"])
        for h in (0, 1):
            lq, ls = T["lq%d" % rd], T["ls%d" % rd]
            for b in range(4):
                mm(4 * h + b, WID[h], T.eq[:, 128 * b:128 * b + 128], T.es[:, 128 * b:128 * b + 128], lq[:, cols(h)], ls[:, cols(h)],
                   ["eq", "lq%d%d" % (rd, h)])
            for b in range(4):
                cp(T.dd[:, 320 * b + AT[h]:320 * b + AT[h] + WID[h]], bank(4 * h + b, WID[h]), ["b%d" % (4 * h + b)], ["dd%d%d" % (h, b)], "av", n=WID[h])
        xn, qn, sn = T["x%d" % rd], T["qx%d" % rd], T["sx%d" % rd]
        for h in (0, 1):
            for t in range(4):
                tt(xn[:, quad(h, t, 4)], T.dd[:, 320 * t:320 * t + 320].indirect(T.mo[:, part(h)]), T.vt[:, quad(h, t, 4)], OP.add,
                   ["mo", "vt%d%d" % (h, t), "dd0%d" % t, "dd1%d" % t] + ["@x"] * h, ["xn%d%d%d" % (rd, h, t)], n=WID[h], x=True)
            quant(qn[:, cols(h)], sn[:, cols(h)], xn[:, quad(h)], state_parts(rd, h), ["qx%d%d" % (rd, h)] + ["@x"] * (1 - h), 4 * WID[h])
            if rd == 3:
                c = cols(h)
                dma("s", [(T.oc[:, quad(h)], qn[:, c].bitcast(dt.uint8))] + [(T.osc[4 * k:4 * k + 4, c], sn[32 * k:32 * k + 4, c]) for k in range(4)],
                    ["qx3%d" % h], [], "oq%d" % h)
            else:
                scores(rd, h)
        if rd < 3:
            flips(rd)
            half_x(rd, 0)
            half_x(rd, 1)
            natural(rd, rd)
            turn_tables()
            if rd == 1:
                turn_windows()
    natural(3, 3)
    mm(1, 320, T.vq[:], T.vs[:], T.qx3[:], T.sx3[:], ["vq", "qx30", "qx31"])
    cp(T.yb[:], bank(1, 320), ["b1"], ["yb"], "av", n=320)
    dma("s", [(T.y[:], T.yb[:])], ["yb"], [], "oy")
    turn_tables(True)
    for k in (0, 1):
        dma("s", [(T.lr[:, 640 * k:640 * k + 640], T.lout[:, 40 * k:40 * k + 40])], ["lo%da" % k, "lo%db" % k], [], "ol")
    issue()
    need("g", dict(total))
    g.wait_ge(T.sem.lsem, sent[0])
